import numpy as np, ml_dtypes
CORES = [9,25,41,57]
N = 4
import mx_ref
BF = ml_dtypes.bfloat16
def cols(t, e):
    v = np.concatenate([t.reshape(128, -1, 4), np.zeros((128, 1, 4), BF)], axis=1)
    return np.ascontiguousarray(v[:, e]).reshape(128, -1)
def cut(t, i, w=512):
    return t[:, w * i:w * i + w]
def f(rng, *shape):
    return mx_ref.flush((rng.standard_normal(shape, dtype=np.float32) * np.exp2(rng.integers(-2, 3, shape[:-1] + (1,)))).astype(BF))
def wide(rng, *shape, cols=0):
    v = rng.standard_normal(shape, dtype=np.float32) * np.exp2(rng.integers(-12, 13, shape)).astype(np.float32)
    if cols: v *= np.repeat(np.exp2(rng.integers(-cols, cols + 1, shape[:-2] + (1, shape[-1] // 4))) * (rng.random(shape[:-2] + (1, shape[-1] // 4)) > 0.0625), 4, axis=-1).astype(np.float32)
    return mx_ref.flush(v.astype(BF))
P, K, R, O = 512, 32, 4, 2
def bf(v):
    return mx_ref.flush(np.asarray(v, np.float32).astype(BF))
def same(v):
    t = np.zeros((128, 512), BF)
    t[:, :4] = v
    return np.stack([t] * N)
def setup_inputs(rng):
    return {"x": f(rng, N, 128, 4 * P), "u": same(f(rng, 128, 4)), "w": f(rng, N, 128, 512 * O)}
def setup_inputs_ties(rng):
    d = setup_inputs(rng)
    T = (P - K - 1) // 3
    H = T // 2
    shared = f(rng, 128, 4 * H)
    x = []
    for r in range(N):
        pool = np.concatenate([shared, f(rng, 128, 4 * (T + 1 - H))], axis=1)
        e = np.concatenate([np.repeat(np.arange(T), 3), np.full(P - 3 * T, T)])
        x.append(cols(pool, rng.permutation(e)))
    d["x"] = np.stack(x)
    d["u"] = bf(d["u"].astype(np.float32) * np.float32(256))
    return d
def setup_inputs_like(rng):
    d = setup_inputs(rng)
    at = rng.permutation(8)
    size = np.zeros(8)
    size[at] = np.exp2(-3.0 - np.arange(8) // 2)
    d["u"] = same(bf((1 + 0.25 * rng.random((128, 4))) * np.repeat(size, 16)[:, None]))
    side = rng.permutation(N) % 2
    x = []
    for r in range(N):
        c = rng.permutation(np.arange(P) % 8)
        h = np.where(c % 2 == side[r], 1.0, 0.75)
        on = np.repeat(np.arange(8)[:, None] == at[c][None, :], 16, axis=0) * h[None, :]
        x.append(bf((on[:, :, None] * (1 + 0.25 * rng.random((128, P, 4))) + 2.0 ** -8 * rng.standard_normal((128, P, 4))).reshape(128, 4 * P)))
    d["x"] = np.stack(x)
    return d
def setup_inputs_late(rng):
    d = setup_inputs(rng)
    half = (np.arange(128) < 64) ^ bool(rng.integers(0, 2))
    d["u"] = same(bf(2.0 ** 28 * (R - 1.5) * (1 + 0.25 * rng.random((128, 4))) * half[:, None]))
    x = []
    for r in range(N):
        late = rng.permutation(P) < rng.integers(2 * K, P // 2 + 1)
        v = np.where(half, 2.0 ** 22, 2.0 ** 26)[:, None] * np.where(late, -1.0, 1.0)[None, :]
        x.append(bf((v[:, :, None] * (1 + 0.25 * rng.random((128, P, 4)))).reshape(128, 4 * P)))
    d["x"] = np.stack(x)
    return d
def setup_inputs_low(rng):
    d = setup_inputs(rng)
    size = np.full((N, P), 2.0 ** 29)
    for r in range(N):
        e = 32 * int(rng.integers(0, P // 32)) + rng.permutation(32)[:K]
        size[r, e] = 2.0 ** 28
        size[r, e[:int(rng.integers(2, K // 2 + 1))]] = 0
    d["x"] = bf(np.repeat(size, 4, axis=1)[:, None, :] * (1.5 + 0.45 * rng.random((N, 128, 4 * P))))
    d["u"] = same(bf(-2.0 ** 29 * (1.5 + 0.45 * rng.random((128, 4)))))
    return d
def setup_inputs_spread(rng):
    d = setup_inputs(rng)
    d["x"] = wide(rng, N, 128, 4 * P, cols=6)
    d["u"] = same(bf(wide(rng, 128, 4).astype(np.float32) * np.float32(256)))
    return d
def check_inputs(d):
    b = []
    for k in ("x", "u", "w"):
        v = np.abs(d[k].astype(np.float32))
        if not (np.isfinite(v).all() and ((v == 0) | (v >= 2.0 ** -30) & (v <= 2.0 ** 30)).all()): b.append("a value of " + k)
    v = d["u"].astype(np.float32)
    if (v[:, :, 4:] != 0).any(): b.append("u has numbers behind its first column")
    if (v != v[:1]).any(): b.append("u isn't the same on all ranks")
    return b
def reference(x, u, w):
    X = [mx_ref.quantize(np.ascontiguousarray(x[r])) for r in range(N)]
    s = [mx_ref.matmul(mx_ref.quantize(np.ascontiguousarray(u[r])), X[r])[0] + np.float32(0.0) for r in range(N)]
    free = np.ones((N, P), bool)
    ch, se, y = np.zeros((N, R, K), np.float32), np.zeros((N, 1, P), np.float32), np.zeros((N, 128, O * R * 128), np.float32)
    M = []
    for b in range(R):
        best = []
        for r in range(N):
            e = np.argsort(np.where(free[r], -s[r], np.float32(np.inf)), kind="stable")[:K]
            free[r, e] = False
            ch[r, b] = e
            best.append(cols(x[r], e))
        M.append(mx_ref.quantize(np.ascontiguousarray(np.concatenate(best, axis=1))))
        if b < R - 1:
            for r in range(N):
                m = mx_ref.matmul(M[b], X[r]).max(axis=0) + np.float32(0.0)
                s[r] = s[r] - np.float32(0.25) * m
    for r in range(N):
        se[r, 0] = s[r]
        for o in range(O):
            q = mx_ref.quantize(np.ascontiguousarray(cut(w[r], o)))
            for b in range(R):
                i = (o * R + b) * 128
                y[r, :, i:i + 128] = mx_ref.matmul(q, M[b])
    return {"ch": ch, "se": se, "y": y}

@@ -1,0 +1,450 @@
+from concourse.bass import DstId, RemoteDMATransfer
+from concourse.mybir import dt, AluOpType, AxisListType, ActivationFunctionType
+
+OP = AluOpType
+P, K, R, O, N = 512, 32, 4, 2, 4
+CW = 514
+LW = 132
+KAPPA = 2.0 ** -24 * (1.0 + 2.0 ** -10)
+TINY = 2.0 ** -124
+BIG = 9e29
+GONE = -1e29
+SB = (2, 3)
+SC = (3,)
+GW = 1536
+
+
+def score(rank):
+    return 2.0 * rank - 128.0
+
+
+X4 = "float8_e4m3fn_x4"
+SCRATCH = {
+    "uc": ("sbuf", [128, 4], "bfloat16"),
+    "ones": ("sbuf", [128, 128], "bfloat16"),
+    "ut": ("sbuf", [128, 512], "bfloat16"),
+    "uq": ("sbuf", [128, 128], X4),
+    "us": ("sbuf", [128, 128], "uint8"),
+    "xr": ("sbuf", [128, 4 * P], "bfloat16"),
+    "xp": ("sbuf", [128, 4 * P], "bfloat16"),
+    "xe": ("sbuf", [128, 4 * P], "bfloat16"),
+    "xq": ("sbuf", [128, P], X4),
+    "xs": ("sbuf", [128, P], "uint8"),
+    "pq": ("sbuf", [128, P], X4),
+    "ps": ("sbuf", [128, P], "uint8"),
+    "eq": ("sbuf", [128, P], X4),
+    "es": ("sbuf", [128, P], "uint8"),
+    "wr": ("sbuf", [128, 512 * O], "bfloat16"),
+    "wq": ("sbuf", [128, 128 * O], X4),
+    "ws": ("sbuf", [128, 128 * O], "uint8"),
+    "mq": ("sbuf", [128, 128 * R], X4),
+    "ms": ("sbuf", [128, 128 * R], "uint8"),
+    "onef": ("sbuf", [128, 4], "float32"),
+    "big": ("sbuf", [128, 128], "float32"),
+    "mask": ("sbuf", [128, 128], "float32"),
+    "mg": ("sbuf", [128, 4], "float32"),
+    "quart": ("sbuf", [128, 32], "float32"),
+    "i16": ("sbuf", [128, 128], "bfloat16"),
+    "w16": ("sbuf", [128, 8], "int32"),
+    "wand": ("sbuf", [128, 8], "int32"),
+    "nt": ("sbuf", [128, 8], "float32"),
+    "nl": ("sbuf", [128, 8], "bfloat16"),
+    "nh": ("sbuf", [128, 8], "bfloat16"),
+    "bc": ("sbuf", [128, 128 * R], "float32"),
+    "be": ("sbuf", [128, 128 * R], "float32"),
+    "srt": ("sbuf", [128, 128 * R], "float32"),
+    "srh": ("sbuf", [128, 128 * R], "float32"),
+    "row": ("sbuf", [128, P * R], "float32"),
+    "rowe": ("sbuf", [128, 128 * R], "float32"),
+    "dd": ("sbuf", [128, 4 * R], "float32"),
+    "thr": ("sbuf", [128, 16 * R], "float32"),
+    "cmp": ("sbuf", [128, CW * 4 * R], "bfloat16"),
+    "sg1": ("sbuf", [128, GW * R], "bfloat16"),
+    "sg2": ("sbuf", [128, GW * R], "bfloat16"),
+    "acc": ("sbuf", [128, 4 * R], "float32"),
+    "acc2": ("sbuf", [128, 4 * R], "float32"),
+    "sc1": ("sbuf", [128, 256 * 4 * R], "bfloat16"),
+    "sc2": ("sbuf", [128, 64 * 4 * R], "bfloat16"),
+    "fl": ("sbuf", [128, 16 * R], "bfloat16"),
+    "ab": ("sbuf", [128, 4 * LW * R], "bfloat16"),
+    "abq": ("sbuf", [128, LW * R], X4),
+    "abs": ("sbuf", [128, LW * R], "uint8"),
+    "off": ("sbuf", [128, 2 * R], "uint16"),
+    "lst": ("sbuf", [128, 2 * R], "float32"),
+    "pen": ("sbuf", [128, 4 * R], "float32"),
+    "srp": ("sbuf", [128, 4 * R], "float32"),
+    "sre": ("sbuf", [128, 4 * R], "float32"),
+    "mx": ("sbuf", [128, 4 * R], "float32"),
+    "me": ("sbuf", [128, 4 * R], "float32"),
+    "mq4": ("sbuf", [128, 4 * R], "float32"),
+    "st": ("sbuf", [128, 4 * R], "float32"),
+    "sf": ("sbuf", [128, 32], "float32"),
+    "sft": ("sbuf", [128, 32], "float32"),
+    "ysb": ("sbuf", [128, O * P], "float32"),
+    "psc": ("psum", [128, 2048], "float32"),
+    "psr": ("psum", [128, 1024], "float32"),
+    "psy": ("psum", [128, 1024], "float32"),
+}
+SEMAPHORES = ["sv", "ss", "sp", "sg", "du", "dx0", "dx1", "dx2", "dx3", "dw", "dsr", "dout",
+              "arr0", "arr1", "arr2", "arr3", "loc"]
+
+
+def rank_program(g, core, T, topo):
+    rank = T.rank_of(core)
+    if rank is None:
+        return
+    AF = ActivationFunctionType
+    queue = {"V": g.vector, "S": g.scalar, "P": g.tensor, "G": g, "Y": g.sync}
+    own = {"V": "sv", "S": "ss", "P": "sp", "G": "sg"}
+    count, seen = {}, {}
+
+    def need(e, deps):
+        for s, v in deps:
+            if seen.get((e, s), 0) < v:
+                queue[e].wait_ge(T.sem[s], v)
+                seen[(e, s)] = v
+
+    def done(e, ins):
+        s = own[e]
+        count[s] = count.get(s, 0) + 1
+        ins.then_inc(T.sem[s], 1)
+        return (s, count[s])
+
+    def dma(e, out, in_, sem, deps=()):
+        need(e, deps)
+        count[sem] = count.get(sem, 0) + 16
+        queue[e].dma_start(out, in_).then_inc(T.sem[sem], 16)
+        return (sem, count[sem])
+
+    def ts(deps, out, in0, s1, s2, op0, op1=None):
+        need("V", deps)
+        if op1 is None:
+            return done("V", g.vector.tensor_scalar(out, in0, s1, s2, op0))
+        return done("V", g.vector.tensor_scalar(out, in0, s1, s2, op0, op1))
+
+    def tt(deps, out, in0, in1, op):
+        need("V", deps)
+        return done("V", g.vector.tensor_tensor(out, in0, in1, op))
+
+    def cp(deps, out, in_):
+        need("V", deps)
+        return done("V", g.vector.tensor_copy(out, in_))
+
+    def turn(deps, out, in_):
+        need("V", deps)
+        return done("V", g.vector.transpose(out, in_))
+
+    def scan(deps, out, d0, d1, init):
+        need("V", deps)
+        return done("V", g.vector.tensor_tensor_scan(out, d0, d1, init, OP.add, OP.add))
+
+    def rmax(deps, out, in_):
+        need("V", deps)
+        return done("V", g.vector.tensor_reduce(out, in_, AxisListType.X, OP.max))
+
+    def act(deps, out, in_, func, **kw):
+        need("S", deps)
+        return done("S", g.scalar.activation(out, in_, func, **kw))
+
+    def gneed(deps):
+        need("G", list(deps) + ([("sg", count["sg"])] if "sg" in count else []))
+
+    def fill(ap, v):
+        return done("V", g.vector.memset(ap, v))
+
+    def quant(deps, q, s, a, n, src, sa):
+        need("V", deps)
+        return done("V", g.vector.quantize_mx(q[:, a:a + n], s[:, a:a + n], src[:, sa:sa + 4 * n]))
+
+    def mm(deps, out, l, lq, ls, r, rq, rs, n, start=True, stop=True):
+        need("P", deps)
+        return done("P", g.tensor.matmul_mx(out, lq[:, l:l + 128], ls[:, l:l + 128],
+                                            rq[:, r:r + n], rs[:, r:r + n], start, stop))
+
+    du = dma("Y", T.uc[:], T.u[:, 0:4], "du")
+    dx = [None] * 4
+    for a in range(4):
+        dx[a] = dma("SYSY"[a], T.xr[:, 512 * a:512 * a + 512], T.x[:, 512 * a:512 * a + 512], "dx%d" % a)
+    dw = dma("Y", T.wr[:], T.w[:], "dw", [dx[2], dx[3]])
+
+    t_ones = fill(T.ones[:], 1.0)
+    t_onef = fill(T.onef[:], 1.0)
+    t_big = fill(T.big[:], BIG)
+    t_quart = fill(T.quart[:], -0.25)
+    for a in range(4):
+        gneed([])
+        t_w16 = done("G", g.iota(T.w16[32 * a:32 * a + 32, :], [[0, 2], [32, 4]], 128 * a + 16, 1))
+    gneed([t_onef])
+    t_mg = done("G", g.affine_select(T.mg[:], T.onef[:], [[32, 4]], OP.is_gt, 0.0, 0, -1))
+    for a in range(4):
+        gneed([t_big])
+        v = slice(32 * a, 32 * a + 32)
+        t_mask = done("G", g.affine_select(T.mask[v, :], T.big[v, :], [[0, 4], [1, 32]], OP.is_ge, -BIG, 0, -1))
+    gneed([])
+    t_i16 = done("G", g.iota(T.i16[:], [[0, 8], [2, 16]], int(score(0)), 0, allow_small_or_imprecise_dtypes=True))
+    t_sf = fill(T.sf[:], 0.0)
+    pads = [[64.0 * ((c in SB) + (c in SC and b > 0)) for c in range(4)] for b in range(R)]
+    for b in range(R):
+        for c in range(4):
+            if pads[b][c]:
+                o = CW * (4 * b + c)
+                fill(T.cmp[:, o:o + 2], pads[b][c])
+    t_wand = ts([t_w16], T.wand[:], T.w16[:], 31, None, OP.bitwise_and)
+    t_nl = ts([t_wand], T.nl[:], T.wand[:], -16.0, -1.0 / 32, OP.add, OP.mult)
+    t_nt = tt([], T.nt[:], T.w16[:], T.wand[:], OP.subtract)
+    t_nh = ts([t_nt], T.nh[:], T.nt[:], -1.0 / 32, None, OP.mult)
+
+    for t in range(4):
+        t_ut = ts([du, t_ones], T.ut[:, t:512:4], T.ones[:], T.uc[:, t:t + 1], None, OP.mult)
+    t_uq = quant([t_ut], T.uq, T.us, 0, 128, T.ut, 0)
+
+    t_xq, t_cv, t_cs, t_row = [None] * 4, None, None, [None] * 2
+
+    def natural(a):
+        t_xq[a] = quant([dx[a]], T.xq, T.xs, 128 * a, 128, T.xr, 512 * a)
+
+    def rows(h):
+        t_row[h] = mm([t_xq[2 * h + 1], t_uq], T.psr[:, 512 * h:512 * h + 256], 0, T.uq, T.us, 256 * h, T.xq, T.xs, 256)
+
+    for a in range(4):
+        for c in range(4):
+            out = T.xp[:, 512 * c + 128 * a:512 * c + 128 * a + 128]
+            in_ = T.xr[:, 512 * a + 128 * c:512 * a + 128 * c + 128]
+            if c < 2:
+                t_cv = cp([dx[a]], out, in_)
+            else:
+                t_cs = act([dx[a]], out, in_, AF.Copy)
+        if a < 3:
+            natural(a)
+        if a == 1:
+            rows(0)
+    t_pq, t_col, t_b4, t_srt = [None] * 4, [None] * 4, [None] * 4, None
+    for c in range(4):
+        t_pq[c] = quant([t_cv if c < 2 else t_cs], T.pq, T.ps, 128 * c, 128, T.xp, 512 * c)
+        t_col[c] = mm([t_pq[c], t_uq], T.psc[:, 512 * c:512 * c + 128], 128 * c, T.pq, T.ps, 0, T.uq, T.us, 128)
+    natural(3)
+    rows(1)
+    for c in range(4):
+        t_b4[c] = cp([t_col[c]], T.bc[:, 32 * c:32 * c + 32], T.psc[:, 512 * c:512 * c + 32])
+        t_srt = turn([], T.srt[:, 32 * c:32 * c + 32], T.psc[:, 512 * c:512 * c + 32])
+    free_c = [t_srt] * 4
+
+    dests = [c for c in T.cores if c != core]
+    mask = topo.mask(core, dests[0])
+    ids = []
+    for c in dests:
+        mask &= topo.mask(core, c)
+        rid, pid, _ = topo.addr(c)
+        ids.append(DstId(rid=rid, pnc=pid))
+    engs = bin(mask).count("1")
+
+    def send(view, b):
+        g.remote_dma_fused([RemoteDMATransfer(dst_ids=ids, dma_engine_mask=mask, remote_sem=T.sem["arr%d" % b],
+                                              srcs=[view], dsts=[view] * len(ids))], local_sem=T.sem.loc)
+
+    t_wq = t_st = t_m = t_srp = t_sre = t_eq = None
+    t_ext = [None] * 4
+    t_y = [None] * O
+    free_y = [None] * O
+    outs = []
+
+    def store(b, o, e):
+        c0 = P * o + 128 * b
+        out, in_ = T.ysb[:, c0:c0 + 128], T.psy[:, 512 * o:512 * o + 128]
+        free_y[o] = cp([t_y[o]], out, in_) if e == "V" else act([t_y[o]], out, in_, AF.Copy)
+        outs.append(dma("Y" if b < R - 1 or o == 0 else "S", T.y[:, c0:c0 + 128], out, "dout", [free_y[o]]))
+
+    for b in range(R):
+        B = 128 * b
+        sc = [T.bc[:, B + 32 * c:B + 32 * c + 1] for c in range(4)]
+        at = [CW * (4 * b + c) for c in range(4)]
+        cor = [at[c] + (2 if pads[b][c] else 0) for c in range(4)]
+        rest = [cor[c] + 128 - 32 * c for c in range(4)]
+        t_d = act(t_b4, T.dd[:, 4 * b:4 * b + 4], T.bc[:, B:B + 128:32], AF.Abs, bias=TINY, scale=KAPPA)
+        for c in range(4):
+            t_thr = act([t_d, t_mg, t_b4[c]], T.thr[:, 16 * b + 4 * c:16 * b + 4 * c + 4], T.mg[:], AF.Identity, bias=sc[c],
+                        scale=T.dd[:, 4 * b + c:4 * b + c + 1])
+        thr = [[T.thr[:, 16 * b + 4 * c + a:16 * b + 4 * c + a + 1] for a in range(4)] for c in range(4)]
+        if b:
+            t_pb = [None] * 4
+            for a in range(3):
+                gneed([t_srt])
+                t_pb[a] = done("G", g.partition_broadcast(T.row[:, P * b + 128 * a:P * b + 128 * a + 128],
+                                                          T.srt[32 * a:32 * a + 1, B:B + 128], 128))
+            row = [T.row[:, P * b + 128 * a:P * b + 128 * a + 128] for a in range(3)] + [T.rowe[:, B:B + 128]]
+            s2, order = 3, [3, 1, 2]
+            t_me, t_be = [None] * 4, None
+            for c in range(4):
+                i = 4 * (b - 1) + c
+                t_me[c] = rmax([t_ext[c]], T.me[:, i:i + 1], T.psc[:, 512 * c:512 * c + 128])
+                t_be = act([t_me[c], t_sre, t_quart], T.be[:, B + 32 * c:B + 32 * c + 32], T.quart[:], AF.Identity,
+                           bias=T.sre[:, i:i + 1], scale=T.me[:, i:i + 1])
+            free_c = t_me
+        else:
+            t_pb = [t_row[a // 2] for a in range(4)]
+            row = [T.psr[:, 512 * (a // 2) + 128 * (a % 2):512 * (a // 2) + 128 * (a % 2) + 128] for a in range(4)]
+            s2, order = 1, [2, 3, 1]
+        for c in range(3):
+            ts([t_srt, t_b4[c]], T.cmp[:, cor[c] + 32:cor[c] + 128 - 32 * c], T.srt[:, B + 32 * c + 32:B + 128], sc[c], -2.0,
+               OP.is_equal, OP.mult)
+        t_srh = tt([t_mask], T.srh[:, B:B + 128], T.srt[:, B:B + 128], T.mask[:], OP.min)
+        if b:
+            t_pb[3] = turn([t_be], T.rowe[:, B:B + 128], T.be[:, B:B + 128])
+        for c in range(4):
+            t_cor = ts([t_srh], T.cmp[:, cor[c]:cor[c] + 32], T.srh[:, B + 32 * c:B + 32 * c + 32], sc[c], -2.0,
+                       OP.is_equal, OP.mult)
+        t_acc = [None] * 4
+        g1 = [GW * b + 256 * c for c in range(4)]
+        sc3 = SC if b else ()
+        t_last = {}
+        for c in range(4):
+            t_sg = act([t_pb[0], t_b4[c]], T.sg1[:, g1[c]:g1[c] + 128], row[0], AF.Sign, bias=sc[c], scale=-1.0)
+        for c in SB:
+            t_sg = act([t_pb[s2], t_thr], T.sg1[:, g1[c] + 128:g1[c] + 256], row[s2], AF.Sign, bias=thr[c][s2], scale=-1.0)
+        t_psr = t_sg
+        for c in range(4):
+            w = 256 if c in SB else 128
+            t_acc[c] = act([t_sg], T.sg2[:, g1[c]:g1[c] + w], T.sg1[:, g1[c]:g1[c] + w], AF.Sign, bias=0.5, scale=-1.0,
+                           accum_out=T.acc[:, 4 * b + c:4 * b + c + 1])
+        g3 = GW * b + 1024
+        for k in range(len(sc3)):
+            t_sg = act([t_pb[2], t_thr], T.sg1[:, g3 + 128 * k:g3 + 128 * k + 128], row[2], AF.Sign, bias=thr[sc3[k]][2],
+                       scale=-1.0)
+        for k in range(len(sc3)):
+            c = sc3[k]
+            t_last[c] = act([t_sg], T.sg2[:, g3 + 128 * k:g3 + 128 * k + 128], T.sg1[:, g3 + 128 * k:g3 + 128 * k + 128],
+                            AF.Sign, bias=0.5, scale=-1.0, accum_out=T.acc2[:, 4 * b + c:4 * b + c + 1])
+        if b:
+            for o in range(O):
+                store(b - 1, o, "S")
+
+        used = [0] * 4
+        t_c = [None] * 4
+
+        def compare(a):
+            for c in range(4):
+                if (a == s2 and c in SB) or (a == order[2] and c in sc3):
+                    continue
+                o = rest[c] + 128 * used[c]
+                used[c] += 1
+                t_c[c] = ts([t_thr, t_pb[a]] + ([t_psr] if b == 0 and a == 1 else []), T.cmp[:, o:o + 128], row[a],
+                            thr[c][a], 2.0, OP.is_ge, OP.mult)
+
+        t_s1 = [None] * 4
+        e1, e2 = [0] * 4, [0] * 4
+
+        def first(c, chunks):
+            n = (rest[c] + 128 * chunks - at[c]) // 2
+            o1 = 256 * (4 * b + c)
+            e1[c], e2[c] = o1 + n - 1, at[c] + 2 * n
+            t_s1[c] = scan([t_c[c], t_acc[c], t_cor], T.sc1[:, o1:o1 + n], T.cmp[:, at[c]:at[c] + n],
+                           T.cmp[:, at[c] + n:at[c] + 2 * n], T.acc[:, 4 * b + c:4 * b + c + 1])
+
+        compare(order[0])
+        compare(order[1])
+        early = list(used)
+        if b:
+            for c in range(4):
+                if c not in SB:
+                    first(c, early[c])
+        compare(order[2])
+        for c in range(4):
+            if t_s1[c] is None:
+                first(c, early[c] if b else used[c] - 1)
+        for c in range(4):
+            o2 = 64 * (4 * b + c)
+            e = e2[c]
+            if c in sc3:
+                t_s2 = tt([t_s1[c], t_last[c]], T.sc2[:, o2 + 63:o2 + 64], T.sc1[:, e1[c]:e1[c] + 1],
+                          T.acc2[:, 4 * b + c:4 * b + c + 1], OP.add)
+            else:
+                t_s2 = scan([t_s1[c], t_c[c]], T.sc2[:, o2:o2 + 64], T.cmp[:, e:e + 64], T.cmp[:, e + 64:e + 128],
+                            T.sc1[:, e1[c]:e1[c] + 1])
+        rk = T.sc2[:, 256 * b + 63:256 * b + 256:64]
+
+        F = 16 * b
+        t_n = ts([t_s2], T.fl[:, F + 4:F + 8], rk, score(16), -32.0, OP.is_ge, OP.mult)
+        t_f = ts([], T.fl[:, F:F + 4], rk, score(16), -32.0, OP.is_lt, OP.mult)
+        if b < R - 1:
+            t_pen = ts([], T.pen[:, 4 * b:4 * b + 4], rk, score(32), GONE, OP.is_lt, OP.mult)
+        t_rm = tt([t_n], T.fl[:, F + 12:F + 16], rk, T.fl[:, F + 4:F + 8], OP.add)
+        A = 4 * LW * b
+        tt([t_f, t_nh, t_nl], T.ab[:, A + 512:A + 520], T.fl[:, F:F + 8], T.nh[:], OP.mult)
+        tt([], T.ab[:, A + 520:A + 528], T.fl[:, F:F + 8], T.nl[:], OP.mult)
+        for t in range(4):
+            t_a = ts([t_rm, t_i16], T.ab[:, A + t:A + 512:4], T.i16[:], T.fl[:, F + 12 + t:F + 13 + t], None, OP.is_equal)
+        if b < R - 1:
+            t_srp = tt([t_pen, t_b4[3]], T.srp[:, 4 * b:4 * b + 4], T.bc[:, B:B + 128:32], T.pen[:, 4 * b:4 * b + 4], OP.add)
+        t_abq = quant([t_a], T.abq, T.abs, LW * b, LW, T.ab, A)
+        L = LW * b
+        mm([t_abq], T.psr[:, 0:128], L, T.abq, T.abs, L + 2, T.abq, T.abs, 128, True, False)
+        t_l = mm([], T.psr[:, 0:128], L, T.abq, T.abs, L + 4, T.abq, T.abs, 128, False, True)
+        t_off = cp([t_l], T.off[:, 2 * b:2 * b + 2], T.psr[:, 126:128])
+
+        m0 = 128 * b + K * rank
+        t_pk = cp([t_off], T.mq[:, m0:m0 + K].bitcast(dt.uint32),
+                  T.xq[:, 0:P].bitcast(dt.uint32).indirect(T.off[:, 2 * b:2 * b + 2]))
+        t_psc = act([t_off], T.ms[:, m0:m0 + K], T.xs[:, 0:P].indirect(T.off[:, 2 * b:2 * b + 2]), AF.Copy)
+        need("G", [t_pk])
+        send(T.mq[:, m0:m0 + K].bitcast(dt.uint8), b)
+        need("G", [t_psc])
+        send(T.ms[:, m0:m0 + K], b)
+
+        t_lst = cp([t_off], T.lst[:, 2 * b:2 * b + 2], T.off[:, 2 * b:2 * b + 2])
+        if b < R - 1:
+            for a in range(4):
+                t_sre = dma("Y", T.sre[32 * a:32 * a + 32, 4 * b:4 * b + 4], T.srp[96:128, 4 * b:4 * b + 4], "dsr", [t_srp])
+        for h in range(2):
+            outs.append(dma("Y", T.ch[b:b + 1, 16 * h:16 * h + 16], T.lst[0:16, 2 * b + h:2 * b + h + 1], "dout", [t_lst]))
+        if b == 0:
+            t_st = cp([t_b4[3]], T.st[:, 0:4], T.bc[:, 0:128:32])
+            for c in range(4):
+                for k in range(4):
+                    t_xe = cp([dx[3]], T.xe[:, 512 * c + 128 * k:512 * c + 128 * k + 128],
+                              T.xr[:, 1536 + 128 * c:1536 + 128 * c + 128])
+            for o in range(O):
+                t_wq = quant([dw], T.wq, T.ws, 128 * o, 128, T.wr, 512 * o)
+            for c in range(4):
+                t_eq = quant([t_xe], T.eq, T.es, 128 * c, 128, T.xe, 512 * c)
+        else:
+            i = 4 * (b - 1)
+            t_q = ts([t_m], T.mq4[:, i:i + 4], T.mx[:, i:i + 4], -0.25, None, OP.mult)
+            if b < R - 1:
+                t_st = tt([t_q, t_st], T.st[:, 4 * b:4 * b + 4], T.mq4[:, i:i + 4], T.st[:, i:i + 4], OP.add)
+            else:
+                t_st = tt([t_q, t_st, t_sf], T.sf[:, 0:4], T.mq4[:, i:i + 4], T.st[:, i:i + 4], OP.add)
+                t_sft = turn([t_st], T.sft[:], T.sf[:])
+                for a in range(4):
+                    outs.append(dma("Y", T.se[0:1, 128 * a:128 * a + 128], T.sft[32 * a:32 * a + 4, :], "dout", [t_sft]))
+
+        arrived = [("arr%d" % b, (N - 1) * 2 * engs), t_pk, t_psc]
+        if b < R - 1:
+            t_mm = [mm(arrived + [free_c[c]], T.psc[:, 512 * c:512 * c + 128], 128 * c, T.pq, T.ps, 128 * b, T.mq, T.ms, 128)
+                    for c in range(4)]
+            t_red = [None] * 4
+            nb = B + 128
+            t_b4 = [None] * 4
+            for c in range(4):
+                i = 4 * b + c
+                m1, s1, out = T.mx[:, i:i + 1], T.srp[:, i:i + 1], T.bc[:, nb + 32 * c:nb + 32 * c + 32]
+                t_red[c] = rmax([t_mm[c]], m1, T.psc[:, 512 * c:512 * c + 128])
+                if c < 3:
+                    t_b4[c] = act([t_red[c], t_srp, t_quart], out, T.quart[:], AF.Identity, bias=s1, scale=m1)
+                else:
+                    t_b4[c] = ts([t_red[c]], out, T.quart[:], m1, s1, OP.mult, OP.add)
+            turn([t_b4[2]], T.srt[:, nb:nb + 96], T.bc[:, nb:nb + 96])
+            t_srt = turn([t_b4[3]], T.srt[:, nb + 96:nb + 128], T.bc[:, nb + 96:nb + 128])
+            t_m = t_red[3]
+            t_ext = [mm([t_red[c], t_eq], T.psc[:, 512 * c:512 * c + 128], 128 * c, T.eq, T.es, 128 * b, T.mq, T.ms, 128)
+                     for c in range(4)]
+        for o in range(O):
+            t_y[o] = mm(arrived + [t_wq] + ([free_y[o]] if free_y[o] else []), T.psy[:, 512 * o:512 * o + 128],
+                        128 * o, T.wq, T.ws, 128 * b, T.mq, T.ms, 128)
+        if b == R - 1:
+            store(b, 0, "V")
+            store(b, 1, "S")
+
+    need("Y", [outs[-1]])
+    need("G", [("loc", 2 * R * engs)])
+    for s in ("sv", "ss", "sp", "sg"):
+        need("Y", [(s, count[s])])

@@ -3,89 +3,32 @@ from concourse.mybir import dt, AluOpType, AxisListType, ActivationFunctionType
 
 OP = AluOpType
 P, K, R, O, N = 512, 32, 4, 2, 4
-CW = 514
+PIECE = (0, 2, 1, 3)
 LW = 132
 KAPPA = 2.0 ** -24 * (1.0 + 2.0 ** -10)
 TINY = 2.0 ** -124
-BIG = 9e29
+LOW = -9e29
 GONE = -1e29
-SB = (2, 3)
-SC = (3,)
-GW = 1536
+STEP = 4096.0
 
 
-def score(rank):
-    return 2.0 * rank - 128.0
+def _sbuf(dtype, **widths):
+    return {name: ("sbuf", [128, w], dtype) for name, w in widths.items()}
 
 
-X4 = "float8_e4m3fn_x4"
 SCRATCH = {
-    "uc": ("sbuf", [128, 4], "bfloat16"),
-    "ones": ("sbuf", [128, 128], "bfloat16"),
-    "ut": ("sbuf", [128, 512], "bfloat16"),
-    "uq": ("sbuf", [128, 128], X4),
-    "us": ("sbuf", [128, 128], "uint8"),
-    "xr": ("sbuf", [128, 4 * P], "bfloat16"),
-    "xp": ("sbuf", [128, 4 * P], "bfloat16"),
-    "xe": ("sbuf", [128, 4 * P], "bfloat16"),
-    "xq": ("sbuf", [128, P], X4),
-    "xs": ("sbuf", [128, P], "uint8"),
-    "pq": ("sbuf", [128, P], X4),
-    "ps": ("sbuf", [128, P], "uint8"),
-    "eq": ("sbuf", [128, P], X4),
-    "es": ("sbuf", [128, P], "uint8"),
-    "wr": ("sbuf", [128, 512 * O], "bfloat16"),
-    "wq": ("sbuf", [128, 128 * O], X4),
-    "ws": ("sbuf", [128, 128 * O], "uint8"),
-    "mq": ("sbuf", [128, 128 * R], X4),
-    "ms": ("sbuf", [128, 128 * R], "uint8"),
-    "onef": ("sbuf", [128, 4], "float32"),
-    "big": ("sbuf", [128, 128], "float32"),
-    "mask": ("sbuf", [128, 128], "float32"),
-    "mg": ("sbuf", [128, 4], "float32"),
-    "quart": ("sbuf", [128, 32], "float32"),
-    "i16": ("sbuf", [128, 128], "bfloat16"),
-    "w16": ("sbuf", [128, 8], "int32"),
-    "wand": ("sbuf", [128, 8], "int32"),
-    "nt": ("sbuf", [128, 8], "float32"),
-    "nl": ("sbuf", [128, 8], "bfloat16"),
-    "nh": ("sbuf", [128, 8], "bfloat16"),
-    "bc": ("sbuf", [128, 128 * R], "float32"),
-    "be": ("sbuf", [128, 128 * R], "float32"),
-    "srt": ("sbuf", [128, 128 * R], "float32"),
-    "srh": ("sbuf", [128, 128 * R], "float32"),
-    "row": ("sbuf", [128, P * R], "float32"),
-    "rowe": ("sbuf", [128, 128 * R], "float32"),
-    "dd": ("sbuf", [128, 4 * R], "float32"),
-    "thr": ("sbuf", [128, 16 * R], "float32"),
-    "cmp": ("sbuf", [128, CW * 4 * R], "bfloat16"),
-    "sg1": ("sbuf", [128, GW * R], "bfloat16"),
-    "sg2": ("sbuf", [128, GW * R], "bfloat16"),
-    "acc": ("sbuf", [128, 4 * R], "float32"),
-    "acc2": ("sbuf", [128, 4 * R], "float32"),
-    "sc1": ("sbuf", [128, 256 * 4 * R], "bfloat16"),
-    "sc2": ("sbuf", [128, 64 * 4 * R], "bfloat16"),
-    "fl": ("sbuf", [128, 16 * R], "bfloat16"),
-    "ab": ("sbuf", [128, 4 * LW * R], "bfloat16"),
-    "abq": ("sbuf", [128, LW * R], X4),
-    "abs": ("sbuf", [128, LW * R], "uint8"),
-    "off": ("sbuf", [128, 2 * R], "uint16"),
-    "lst": ("sbuf", [128, 2 * R], "float32"),
-    "pen": ("sbuf", [128, 4 * R], "float32"),
-    "srp": ("sbuf", [128, 4 * R], "float32"),
-    "sre": ("sbuf", [128, 4 * R], "float32"),
-    "mx": ("sbuf", [128, 4 * R], "float32"),
-    "me": ("sbuf", [128, 4 * R], "float32"),
-    "mq4": ("sbuf", [128, 4 * R], "float32"),
-    "st": ("sbuf", [128, 4 * R], "float32"),
-    "sf": ("sbuf", [128, 32], "float32"),
-    "sft": ("sbuf", [128, 32], "float32"),
-    "ysb": ("sbuf", [128, O * P], "float32"),
+    **_sbuf("bfloat16", uc=4, ones=128, ut=512, xr=4 * P, xp=4 * P, wr=512 * O, i32=32, i16=256, cmp=P * R, en=128 * R,
+            ent=128 * R, cm2=96 * R, r2=48 * R, hb=2 * R, ab=4 * LW, fl=32 * R, flt=32 * R),
+    **_sbuf("float8_e4m3fn_x4", xq=P, pq=P, wq=128 * O, mq=128 * (R + 1), abq=LW),
+    **_sbuf("uint8", xs=P, ps=P, ws=128 * O, ms=128 * (R + 1), abs=LW),
+    **_sbuf("float32", tri=32, quart=32, low=96, num=P, at=4, base=1, zero=2, bc=128 * R, srt=128 * R, th=128 * R,
+            dd=4 * R, rs=256 * R, ev=128 * R, evt=192, vs=96 * R, enj=128 * R, p4=R, gg=64 * R, chs=K * R, cnt=R,
+            pen=4 * R, srp=4 * R, mo=4 * R, mx=384 * R, mq4=4 * R, st=4 * R, sf=32, sft=32, ysb=O * P),
+    **_sbuf("uint16", off=2 * R),
     "psc": ("psum", [128, 2048], "float32"),
-    "psr": ("psum", [128, 1024], "float32"),
-    "psy": ("psum", [128, 1024], "float32"),
+    "psr": ("psum", [128, 2048], "float32"),
 }
-SEMAPHORES = ["sv", "ss", "sp", "sg", "du", "dx0", "dx1", "dx2", "dx3", "dw", "dsr", "dout",
+SEMAPHORES = ["sv", "ss", "sp", "sg", "du", "dx0", "dx1", "dx2", "dx3", "dw", "dout",
               "arr0", "arr1", "arr2", "arr3", "loc"]
 
 
@@ -134,23 +77,24 @@ def rank_program(g, core, T, topo):
         need("V", deps)
         return done("V", g.vector.transpose(out, in_))
 
-    def scan(deps, out, d0, d1, init):
+    def scan(deps, out, d0, d1, init, op0, op1):
         need("V", deps)
-        return done("V", g.vector.tensor_tensor_scan(out, d0, d1, init, OP.add, OP.add))
+        return done("V", g.vector.tensor_tensor_scan(out, d0, d1, init, op0, op1))
 
-    def rmax(deps, out, in_):
+    def red(deps, out, in_, op):
         need("V", deps)
-        return done("V", g.vector.tensor_reduce(out, in_, AxisListType.X, OP.max))
+        return done("V", g.vector.tensor_reduce(out, in_, AxisListType.X, op))
 
     def act(deps, out, in_, func, **kw):
         need("S", deps)
         return done("S", g.scalar.activation(out, in_, func, **kw))
 
-    def gneed(deps):
-        need("G", list(deps) + ([("sg", count["sg"])] if "sg" in count else []))
-
     def fill(ap, v):
         return done("V", g.vector.memset(ap, v))
+
+    def whole(out, pattern, step):
+        need("G", [("sg", count.get("sg", 0))])
+        return done("G", g.iota(out, pattern, 0, step, allow_small_or_imprecise_dtypes=True))
 
     def quant(deps, q, s, a, n, src, sa):
         need("V", deps)
@@ -161,6 +105,9 @@ def rank_program(g, core, T, topo):
         return done("P", g.tensor.matmul_mx(out, lq[:, l:l + 128], ls[:, l:l + 128],
                                             rq[:, r:r + n], rs[:, r:r + n], start, stop))
 
+    quad = [slice(32 * a, 32 * a + 32) for a in range(4)]
+    half = [slice(0, 64), slice(64, 128)]
+
     du = dma("Y", T.uc[:], T.u[:, 0:4], "du")
     dx = [None] * 4
     for a in range(4):
@@ -168,66 +115,46 @@ def rank_program(g, core, T, topo):
     dw = dma("Y", T.wr[:], T.w[:], "dw", [dx[2], dx[3]])
 
     t_ones = fill(T.ones[:], 1.0)
-    t_onef = fill(T.onef[:], 1.0)
-    t_big = fill(T.big[:], BIG)
-    t_quart = fill(T.quart[:], -0.25)
+    fill(T.quart[:], -0.25)
+    fill(T.low[:], LOW)
+    fill(T.zero[:], 0.0)
+    fill(T.sf[:], 0.0)
+    fill(T.evt[:], 0.0)
+    fill(T.ab[:], 0.0)
     for a in range(4):
-        gneed([])
-        t_w16 = done("G", g.iota(T.w16[32 * a:32 * a + 32, :], [[0, 2], [32, 4]], 128 * a + 16, 1))
-    gneed([t_onef])
-    t_mg = done("G", g.affine_select(T.mg[:], T.onef[:], [[32, 4]], OP.is_gt, 0.0, 0, -1))
+        fill(T.base[quad[a], :], 128.0 * PIECE[a] - STEP)
     for a in range(4):
-        gneed([t_big])
-        v = slice(32 * a, 32 * a + 32)
-        t_mask = done("G", g.affine_select(T.mask[v, :], T.big[v, :], [[0, 4], [1, 32]], OP.is_ge, -BIG, 0, -1))
-    gneed([])
-    t_i16 = done("G", g.iota(T.i16[:], [[0, 8], [2, 16]], int(score(0)), 0, allow_small_or_imprecise_dtypes=True))
-    t_sf = fill(T.sf[:], 0.0)
-    pads = [[64.0 * ((c in SB) + (c in SC and b > 0)) for c in range(4)] for b in range(R)]
-    for b in range(R):
-        for c in range(4):
-            if pads[b][c]:
-                o = CW * (4 * b + c)
-                fill(T.cmp[:, o:o + 2], pads[b][c])
-    t_wand = ts([t_w16], T.wand[:], T.w16[:], 31, None, OP.bitwise_and)
-    t_nl = ts([t_wand], T.nl[:], T.wand[:], -16.0, -1.0 / 32, OP.add, OP.mult)
-    t_nt = tt([], T.nt[:], T.w16[:], T.wand[:], OP.subtract)
-    t_nh = ts([t_nt], T.nh[:], T.nt[:], -1.0 / 32, None, OP.mult)
+        whole(T.at[quad[a], :], [[32, 4]], 1)
+    t_i32 = whole(T.i32[:], [[1, 32]], 0)
+    t_i16 = whole(T.i16[:], [[16, 2], [0, 8], [1, 16]], 0)
+    t_num = whole(T.num[:], [[1, P]], 0)
 
     for t in range(4):
         t_ut = ts([du, t_ones], T.ut[:, t:512:4], T.ones[:], T.uc[:, t:t + 1], None, OP.mult)
-    t_uq = quant([t_ut], T.uq, T.us, 0, 128, T.ut, 0)
 
-    t_xq, t_cv, t_cs, t_row = [None] * 4, None, None, [None] * 2
-
-    def natural(a):
-        t_xq[a] = quant([dx[a]], T.xq, T.xs, 128 * a, 128, T.xr, 512 * a)
-
-    def rows(h):
-        t_row[h] = mm([t_xq[2 * h + 1], t_uq], T.psr[:, 512 * h:512 * h + 256], 0, T.uq, T.us, 256 * h, T.xq, T.xs, 256)
-
-    for a in range(4):
+    def reorder(a):
+        j = PIECE[a]
         for c in range(4):
-            out = T.xp[:, 512 * c + 128 * a:512 * c + 128 * a + 128]
-            in_ = T.xr[:, 512 * a + 128 * c:512 * a + 128 * c + 128]
-            if c < 2:
-                t_cv = cp([dx[a]], out, in_)
-            else:
-                t_cs = act([dx[a]], out, in_, AF.Copy)
-        if a < 3:
-            natural(a)
-        if a == 1:
-            rows(0)
-    t_pq, t_col, t_b4, t_srt = [None] * 4, [None] * 4, [None] * 4, None
-    for c in range(4):
-        t_pq[c] = quant([t_cv if c < 2 else t_cs], T.pq, T.ps, 128 * c, 128, T.xp, 512 * c)
-        t_col[c] = mm([t_pq[c], t_uq], T.psc[:, 512 * c:512 * c + 128], 128 * c, T.pq, T.ps, 0, T.uq, T.us, 128)
-    natural(3)
-    rows(1)
-    for c in range(4):
-        t_b4[c] = cp([t_col[c]], T.bc[:, 32 * c:32 * c + 32], T.psc[:, 512 * c:512 * c + 32])
-        t_srt = turn([], T.srt[:, 32 * c:32 * c + 32], T.psc[:, 512 * c:512 * c + 32])
-    free_c = [t_srt] * 4
+            t = act([dx[j]], T.xp[:, 512 * c + 128 * a:512 * c + 128 * a + 128],
+                    T.xr[:, 512 * j + 128 * c:512 * j + 128 * c + 128], AF.Copy)
+        return t
+
+    t_m = [None] * 4
+    for a in range(4):
+        j = PIECE[a]
+        t_xq = quant([dx[j]], T.xq, T.xs, 128 * j, 128, T.xr, 512 * j)
+        if a == 0:
+            t_uq = quant([t_ut], T.mq, T.ms, 0, 128, T.ut, 0)
+            reorder(0)
+        t_m[a] = mm([t_xq, t_uq], T.psc[:, 512 * a:512 * a + 128], 0, T.mq, T.ms, 128 * j, T.xq, T.xs, 128)
+        t_m2 = mm([], T.psr[:, 512 * a:512 * a + 128], 0, T.mq, T.ms, 128 * j, T.xq, T.xs, 128)
+        t_row = act([t_m2], T.srt[quad[a], 0:128], T.psr[quad[a], 512 * a:512 * a + 128], AF.Copy)
+    for a in range(4):
+        if a == 3:
+            t_tri = ts([t_i32], T.tri[:], T.i32[:], T.at[:, 0:1], None, OP.is_ge)
+        t_turn = turn([t_m[a]], T.bc[quad[a], 0:128], T.psc[quad[a], 512 * a:512 * a + 128])
+    t_b4 = [t_turn] * 4
+    t_srt = [t_row] * 2
 
     dests = [c for c in T.cores if c != core]
     mask = topo.mask(core, dests[0])
@@ -238,208 +165,158 @@ def rank_program(g, core, T, topo):
         ids.append(DstId(rid=rid, pnc=pid))
     engs = bin(mask).count("1")
 
-    def send(view, b):
-        g.remote_dma_fused([RemoteDMATransfer(dst_ids=ids, dma_engine_mask=mask, remote_sem=T.sem["arr%d" % b],
-                                              srcs=[view], dsts=[view] * len(ids))], local_sem=T.sem.loc)
+    def place(b, sender, holder):
+        return 128 * (b + 1) + K * ((sender - holder) % N if b < R - 1 else sender)
 
-    t_wq = t_st = t_m = t_srp = t_sre = t_eq = None
-    t_ext = [None] * 4
+    def send(buf, b, codes):
+        views = [buf[:, place(b, rank, T.rank_of(c)):place(b, rank, T.rank_of(c)) + K] for c in [core] + dests]
+        if codes:
+            views = [v.bitcast(dt.uint8) for v in views]
+        g.remote_dma_fused([RemoteDMATransfer(dst_ids=ids, dma_engine_mask=mask, remote_sem=T.sem["arr%d" % b],
+                                              srcs=views[:1], dsts=views[1:])], local_sem=T.sem.loc)
+
+    t_wq = t_st = None
     t_y = [None] * O
     free_y = [None] * O
     outs = []
+    psy = [T.psr[:, 1024 + 512 * o:1024 + 512 * o + 128] for o in range(O)]
 
     def store(b, o, e):
         c0 = P * o + 128 * b
-        out, in_ = T.ysb[:, c0:c0 + 128], T.psy[:, 512 * o:512 * o + 128]
-        free_y[o] = cp([t_y[o]], out, in_) if e == "V" else act([t_y[o]], out, in_, AF.Copy)
-        outs.append(dma("Y" if b < R - 1 or o == 0 else "S", T.y[:, c0:c0 + 128], out, "dout", [free_y[o]]))
+        out = T.ysb[:, c0:c0 + 128]
+        free_y[o] = cp([t_y[o]], out, psy[o]) if e == "V" else act([t_y[o]], out, psy[o], AF.Copy)
+        cut = K * rank if b < R - 1 else 0
+        q = "Y" if b < R - 1 or o == 0 else "S"
+        outs.append(dma(q, T.y[:, c0 + cut:c0 + 128], T.ysb[:, c0:c0 + 128 - cut], "dout", [free_y[o]]))
+        if cut:
+            outs.append(dma(q, T.y[:, c0:c0 + cut], T.ysb[:, c0 + 128 - cut:c0 + 128], "dout"))
 
     for b in range(R):
         B = 128 * b
         sc = [T.bc[:, B + 32 * c:B + 32 * c + 1] for c in range(4)]
-        at = [CW * (4 * b + c) for c in range(4)]
-        cor = [at[c] + (2 if pads[b][c] else 0) for c in range(4)]
-        rest = [cor[c] + 128 - 32 * c for c in range(4)]
         t_d = act(t_b4, T.dd[:, 4 * b:4 * b + 4], T.bc[:, B:B + 128:32], AF.Abs, bias=TINY, scale=KAPPA)
-        for c in range(4):
-            t_thr = act([t_d, t_mg, t_b4[c]], T.thr[:, 16 * b + 4 * c:16 * b + 4 * c + 4], T.mg[:], AF.Identity, bias=sc[c],
-                        scale=T.dd[:, 4 * b + c:4 * b + c + 1])
-        thr = [[T.thr[:, 16 * b + 4 * c + a:16 * b + 4 * c + a + 1] for a in range(4)] for c in range(4)]
-        if b:
-            t_pb = [None] * 4
-            for a in range(3):
-                gneed([t_srt])
-                t_pb[a] = done("G", g.partition_broadcast(T.row[:, P * b + 128 * a:P * b + 128 * a + 128],
-                                                          T.srt[32 * a:32 * a + 1, B:B + 128], 128))
-            row = [T.row[:, P * b + 128 * a:P * b + 128 * a + 128] for a in range(3)] + [T.rowe[:, B:B + 128]]
-            s2, order = 3, [3, 1, 2]
-            t_me, t_be = [None] * 4, None
-            for c in range(4):
-                i = 4 * (b - 1) + c
-                t_me[c] = rmax([t_ext[c]], T.me[:, i:i + 1], T.psc[:, 512 * c:512 * c + 128])
-                t_be = act([t_me[c], t_sre, t_quart], T.be[:, B + 32 * c:B + 32 * c + 32], T.quart[:], AF.Identity,
-                           bias=T.sre[:, i:i + 1], scale=T.me[:, i:i + 1])
-            free_c = t_me
-        else:
-            t_pb = [t_row[a // 2] for a in range(4)]
-            row = [T.psr[:, 512 * (a // 2) + 128 * (a % 2):512 * (a // 2) + 128 * (a % 2) + 128] for a in range(4)]
-            s2, order = 1, [2, 3, 1]
-        for c in range(3):
-            ts([t_srt, t_b4[c]], T.cmp[:, cor[c] + 32:cor[c] + 128 - 32 * c], T.srt[:, B + 32 * c + 32:B + 128], sc[c], -2.0,
-               OP.is_equal, OP.mult)
-        t_srh = tt([t_mask], T.srh[:, B:B + 128], T.srt[:, B:B + 128], T.mask[:], OP.min)
-        if b:
-            t_pb[3] = turn([t_be], T.rowe[:, B:B + 128], T.be[:, B:B + 128])
-        for c in range(4):
-            t_cor = ts([t_srh], T.cmp[:, cor[c]:cor[c] + 32], T.srh[:, B + 32 * c:B + 32 * c + 32], sc[c], -2.0,
-                       OP.is_equal, OP.mult)
-        t_acc = [None] * 4
-        g1 = [GW * b + 256 * c for c in range(4)]
-        sc3 = SC if b else ()
-        t_last = {}
-        for c in range(4):
-            t_sg = act([t_pb[0], t_b4[c]], T.sg1[:, g1[c]:g1[c] + 128], row[0], AF.Sign, bias=sc[c], scale=-1.0)
-        for c in SB:
-            t_sg = act([t_pb[s2], t_thr], T.sg1[:, g1[c] + 128:g1[c] + 256], row[s2], AF.Sign, bias=thr[c][s2], scale=-1.0)
-        t_psr = t_sg
-        for c in range(4):
-            w = 256 if c in SB else 128
-            t_acc[c] = act([t_sg], T.sg2[:, g1[c]:g1[c] + w], T.sg1[:, g1[c]:g1[c] + w], AF.Sign, bias=0.5, scale=-1.0,
-                           accum_out=T.acc[:, 4 * b + c:4 * b + c + 1])
-        g3 = GW * b + 1024
-        for k in range(len(sc3)):
-            t_sg = act([t_pb[2], t_thr], T.sg1[:, g3 + 128 * k:g3 + 128 * k + 128], row[2], AF.Sign, bias=thr[sc3[k]][2],
-                       scale=-1.0)
-        for k in range(len(sc3)):
-            c = sc3[k]
-            t_last[c] = act([t_sg], T.sg2[:, g3 + 128 * k:g3 + 128 * k + 128], T.sg1[:, g3 + 128 * k:g3 + 128 * k + 128],
-                            AF.Sign, bias=0.5, scale=-1.0, accum_out=T.acc2[:, 4 * b + c:4 * b + c + 1])
+        t_th = [act([t_d, t_tri], T.th[:, B + 32 * c:B + 32 * c + 32], T.tri[:], AF.Identity, bias=sc[c],
+                    scale=T.dd[:, 4 * b + c:4 * b + c + 1]) for c in range(4)]
         if b:
             for o in range(O):
                 store(b - 1, o, "S")
-
-        used = [0] * 4
-        t_c = [None] * 4
-
-        def compare(a):
-            for c in range(4):
-                if (a == s2 and c in SB) or (a == order[2] and c in sc3):
-                    continue
-                o = rest[c] + 128 * used[c]
-                used[c] += 1
-                t_c[c] = ts([t_thr, t_pb[a]] + ([t_psr] if b == 0 and a == 1 else []), T.cmp[:, o:o + 128], row[a],
-                            thr[c][a], 2.0, OP.is_ge, OP.mult)
-
-        t_s1 = [None] * 4
-        e1, e2 = [0] * 4, [0] * 4
-
-        def first(c, chunks):
-            n = (rest[c] + 128 * chunks - at[c]) // 2
-            o1 = 256 * (4 * b + c)
-            e1[c], e2[c] = o1 + n - 1, at[c] + 2 * n
-            t_s1[c] = scan([t_c[c], t_acc[c], t_cor], T.sc1[:, o1:o1 + n], T.cmp[:, at[c]:at[c] + n],
-                           T.cmp[:, at[c] + n:at[c] + 2 * n], T.acc[:, 4 * b + c:4 * b + c + 1])
-
-        compare(order[0])
-        compare(order[1])
-        early = list(used)
-        if b:
-            for c in range(4):
-                if c not in SB:
-                    first(c, early[c])
-        compare(order[2])
-        for c in range(4):
-            if t_s1[c] is None:
-                first(c, early[c] if b else used[c] - 1)
-        for c in range(4):
-            o2 = 64 * (4 * b + c)
-            e = e2[c]
-            if c in sc3:
-                t_s2 = tt([t_s1[c], t_last[c]], T.sc2[:, o2 + 63:o2 + 64], T.sc1[:, e1[c]:e1[c] + 1],
-                          T.acc2[:, 4 * b + c:4 * b + c + 1], OP.add)
-            else:
-                t_s2 = scan([t_s1[c], t_c[c]], T.sc2[:, o2:o2 + 64], T.cmp[:, e:e + 64], T.cmp[:, e + 64:e + 128],
-                            T.sc1[:, e1[c]:e1[c] + 1])
-        rk = T.sc2[:, 256 * b + 63:256 * b + 256:64]
-
-        F = 16 * b
-        t_n = ts([t_s2], T.fl[:, F + 4:F + 8], rk, score(16), -32.0, OP.is_ge, OP.mult)
-        t_f = ts([], T.fl[:, F:F + 4], rk, score(16), -32.0, OP.is_lt, OP.mult)
-        if b < R - 1:
-            t_pen = ts([], T.pen[:, 4 * b:4 * b + 4], rk, score(32), GONE, OP.is_lt, OP.mult)
-        t_rm = tt([t_n], T.fl[:, F + 12:F + 16], rk, T.fl[:, F + 4:F + 8], OP.add)
-        A = 4 * LW * b
-        tt([t_f, t_nh, t_nl], T.ab[:, A + 512:A + 520], T.fl[:, F:F + 8], T.nh[:], OP.mult)
-        tt([], T.ab[:, A + 520:A + 528], T.fl[:, F:F + 8], T.nl[:], OP.mult)
-        for t in range(4):
-            t_a = ts([t_rm, t_i16], T.ab[:, A + t:A + 512:4], T.i16[:], T.fl[:, F + 12 + t:F + 13 + t], None, OP.is_equal)
-        if b < R - 1:
-            t_srp = tt([t_pen, t_b4[3]], T.srp[:, 4 * b:4 * b + 4], T.bc[:, B:B + 128:32], T.pen[:, 4 * b:4 * b + 4], OP.add)
-        t_abq = quant([t_a], T.abq, T.abs, LW * b, LW, T.ab, A)
-        L = LW * b
-        mm([t_abq], T.psr[:, 0:128], L, T.abq, T.abs, L + 2, T.abq, T.abs, 128, True, False)
-        t_l = mm([], T.psr[:, 0:128], L, T.abq, T.abs, L + 4, T.abq, T.abs, 128, False, True)
-        t_off = cp([t_l], T.off[:, 2 * b:2 * b + 2], T.psr[:, 126:128])
-
-        m0 = 128 * b + K * rank
-        t_pk = cp([t_off], T.mq[:, m0:m0 + K].bitcast(dt.uint32),
-                  T.xq[:, 0:P].bitcast(dt.uint32).indirect(T.off[:, 2 * b:2 * b + 2]))
-        t_psc = act([t_off], T.ms[:, m0:m0 + K], T.xs[:, 0:P].indirect(T.off[:, 2 * b:2 * b + 2]), AF.Copy)
-        need("G", [t_pk])
-        send(T.mq[:, m0:m0 + K].bitcast(dt.uint8), b)
-        need("G", [t_psc])
-        send(T.ms[:, m0:m0 + K], b)
-
-        t_lst = cp([t_off], T.lst[:, 2 * b:2 * b + 2], T.off[:, 2 * b:2 * b + 2])
-        if b < R - 1:
-            for a in range(4):
-                t_sre = dma("Y", T.sre[32 * a:32 * a + 32, 4 * b:4 * b + 4], T.srp[96:128, 4 * b:4 * b + 4], "dsr", [t_srp])
-        for h in range(2):
-            outs.append(dma("Y", T.ch[b:b + 1, 16 * h:16 * h + 16], T.lst[0:16, 2 * b + h:2 * b + h + 1], "dout", [t_lst]))
-        if b == 0:
-            t_st = cp([t_b4[3]], T.st[:, 0:4], T.bc[:, 0:128:32])
-            for c in range(4):
-                for k in range(4):
-                    t_xe = cp([dx[3]], T.xe[:, 512 * c + 128 * k:512 * c + 128 * k + 128],
-                              T.xr[:, 1536 + 128 * c:1536 + 128 * c + 128])
-            for o in range(O):
-                t_wq = quant([dw], T.wq, T.ws, 128 * o, 128, T.wr, 512 * o)
-            for c in range(4):
-                t_eq = quant([t_xe], T.eq, T.es, 128 * c, 128, T.xe, 512 * c)
         else:
-            i = 4 * (b - 1)
-            t_q = ts([t_m], T.mq4[:, i:i + 4], T.mx[:, i:i + 4], -0.25, None, OP.mult)
-            if b < R - 1:
-                t_st = tt([t_q, t_st], T.st[:, 4 * b:4 * b + 4], T.mq4[:, i:i + 4], T.st[:, i:i + 4], OP.add)
-            else:
-                t_st = tt([t_q, t_st, t_sf], T.sf[:, 0:4], T.mq4[:, i:i + 4], T.st[:, i:i + 4], OP.add)
-                t_sft = turn([t_st], T.sft[:], T.sf[:])
-                for a in range(4):
-                    outs.append(dma("Y", T.se[0:1, 128 * a:128 * a + 128], T.sft[32 * a:32 * a + 4, :], "dout", [t_sft]))
+            reorder(1)
+            reorder(2)
+        C, i = P * b, 4 * b
+        for c, lo in ((1, 1), (2, 1), (0, 0), (1, 0), (2, 0), (3, 1)):
+            j0, j1 = (0, 32 * c) if lo else (32 * c + 32, 128)
+            ts([t_srt[int(j1 > 64)]] + t_b4, T.cmp[:, C + 128 * c + j0:C + 128 * c + j1], T.srt[:, B + j0:B + j1], sc[c],
+               None, OP.is_ge if lo else OP.is_gt)
+        t_c = [tt([t_th[c]], T.cmp[:, C + 160 * c:C + 160 * c + 32], T.srt[:, B + 32 * c:B + 32 * c + 32],
+                  T.th[:, B + 32 * c:B + 32 * c + 32], OP.is_ge) for c in range(4)]
+        S = 256 * b
+        t_rs = [scan([t_c[c]], T.rs[:, S + 64 * c:S + 64 * c + 64], T.cmp[:, C + 128 * c:C + 128 * c + 64],
+                     T.cmp[:, C + 128 * c + 64:C + 128 * c + 128], 0.0, OP.add, OP.add) for c in range(4)]
+        r1 = [T.rs[:, S + 64 * c + 63:S + 64 * c + 64] for c in range(4)]
+        t_ev = [ts([t_rs[c]], T.ev[:, B + 32 * c:B + 32 * c + 32], T.i32[:], r1[c], sc[c], OP.is_equal, OP.mult)
+                for c in range(4)]
+        for c in range(4):
+            t_en = ts([], T.en[:, B + 32 * c:B + 32 * c + 32], T.i32[:], r1[c], T.at[:, c:c + 1], OP.is_equal, OP.mult)
+        for h in range(2):
+            t_evt = turn([t_ev[2 * h + 1]], T.evt[:, 96 * h:96 * h + 64], T.ev[:, B + 64 * h:B + 64 * h + 64])
+        t_ent = turn([t_en], T.ent[:, B:B + 128], T.en[:, B:B + 128])
+        G, H = 96 * b, 64 * b
+        t_vs = scan([t_evt], T.vs[:, G:G + 96], T.evt[:, 0:96], T.evt[:, 96:192], 0.0, OP.add, OP.add)
+        p4, hb = T.p4[:, b:b + 1], T.hb[:, 2 * b:2 * b + 2]
+        t_p4 = act([t_ent], T.enj[:, B:B + 128], T.ent[:, B:B + 128], AF.Identity, bias=STEP / 128, accum_out=p4)
+        t_hb = act([t_p4], hb, T.zero[:], AF.Identity, bias=p4)
+        act([t_hb], T.ab[:, 512:518:5], hb, AF.Identity, bias=T.base[:])
+        t_lo = act([], T.ab[:, 520:526:5], hb, AF.Identity, bias=p4, scale=-1.0)
+        if b == 0:
+            t_xp = reorder(3)
+
+        t_g = [turn([t_vs], T.gg[:, H:H + 32], T.vs[:, G + 64:G + 96])]
+        t_g += [turn([], T.gg[half[h], H + 32:H + 64], T.vs[half[1 - h], G + 64:G + 96]) for h in range(2)]
+        for h in range(2):
+            ts(t_g[:1], T.cm2[half[h], G:G + 32], T.gg[half[1 - h], H:H + 32], T.vs[half[h], G + 95:G + 96], None,
+               OP.is_ge if h else OP.is_gt)
+        for a in range(4):
+            t_c2 = ts([t_g[1 + a // 2]], T.cm2[quad[a], G + 32:G + 96], T.gg[quad[a ^ 1], H:H + 64],
+                      T.vs[quad[a], G + 95:G + 96], None, OP.is_ge if a & 1 else OP.is_gt)
+        t_r2 = scan([t_c2], T.r2[:, 48 * b:48 * b + 48], T.cm2[:, G:G + 48], T.cm2[:, G + 48:G + 96], T.at[:, 0:1],
+                    OP.add, OP.add)
+        rk = T.r2[:, 48 * b + 47:48 * b + 48]
+
+        for h in range(2):
+            t_a = ts([t_r2, t_i16], T.ab[:, h:512:4], T.i16[:, 128 * h:128 * h + 128], rk, None, OP.is_equal)
+        if b < R - 1:
+            t_fl = ts([], T.fl[:, 32 * b:32 * b + 32], T.ones[:, 0:32], rk, float(K), OP.mult, OP.is_lt)
+        t_abq = quant([t_a, t_lo], T.abq, T.abs, 0, LW, T.ab, 0)
+        mm([t_abq], T.psr[:, 0:128], 0, T.abq, T.abs, 2, T.abq, T.abs, 128, True, False)
+        t_l = mm([], T.psr[:, 0:128], 0, T.abq, T.abs, 4, T.abq, T.abs, 128, False, True)
+        if b < R - 1:
+            t_flt = turn([t_fl], T.flt[:, 32 * b:32 * b + 32], T.fl[:, 32 * b:32 * b + 32])
+            if b == 0:
+                quant([t_xp], T.pq, T.ps, 0, 256, T.xp, 0)
+            t_cnt = red([t_flt], T.cnt[:, b:b + 1], T.flt[:, 32 * b:32 * b + 32], OP.add)
+            if b == 0:
+                quant([], T.pq, T.ps, 256, 128, T.xp, 1024)
+        off = T.off[:, 2 * b:2 * b + 2]
+        t_off = cp([t_l], off, T.psr[:, 126:128])
+        if b < R - 1:
+            t_pen = ts([t_cnt], T.pen[:, i:i + 4], T.rs[:, S + 63:S + 256:64], T.cnt[:, b:b + 1], GONE, OP.is_lt, OP.mult)
+        if b == 0:
+            t_pq = quant([], T.pq, T.ps, 384, 128, T.xp, 1536)
+
+        m0 = place(b, rank, rank)
+        t_pk = cp([t_off], T.mq[:, m0:m0 + K].bitcast(dt.uint32), T.xq[:, 0:P].bitcast(dt.uint32).indirect(off))
+        t_psc = act([t_off], T.ms[:, m0:m0 + K], T.xs[:, 0:P].indirect(off), AF.Copy)
+        need("G", [t_pk])
+        send(T.mq, b, True)
+        need("G", [t_psc])
+        send(T.ms, b, False)
+
+        t_ch = act([t_num], T.chs[:, K * b:K * b + K], T.num[:, 0:P].indirect(off), AF.Copy)
+        if b < R - 1:
+            t_own = [mm([t_pk, t_psc, t_pq], T.psc[:, 512 * c:512 * c + 128], 128 * c, T.pq, T.ps, m0 + K - 128,
+                        T.mq, T.ms, 128) for c in range(4)]
+            t_srp = tt([t_pen], T.srp[:, i:i + 4], T.bc[:, B:B + 128:32], T.pen[:, i:i + 4], OP.add)
+            if b == 0:
+                t_st = cp([], T.st[:, 0:4], T.bc[:, 0:128:32])
+                t_wq = quant([dw], T.wq, T.ws, 0, 128 * O, T.wr, 0)
+            t_mo = [red([t_own[c]], T.mo[:, i + c:i + c + 1], T.psc[:, 512 * c + 128 - K:512 * c + 128], OP.max)
+                    for c in range(4)]
+        else:
+            t_sft = turn([t_st], T.sft[:], T.sf[:])
+            outs.append(dma("Y", T.ch[:], T.chs[0:1, :], "dout", [t_ch]))
+            for a in range(4):
+                j = 128 * PIECE[a]
+                outs.append(dma("Y", T.se[0:1, j:j + 128], T.sft[32 * a:32 * a + 4, :], "dout", [t_sft]))
 
         arrived = [("arr%d" % b, (N - 1) * 2 * engs), t_pk, t_psc]
+        M = 128 * (b + 1)
         if b < R - 1:
-            t_mm = [mm(arrived + [free_c[c]], T.psc[:, 512 * c:512 * c + 128], 128 * c, T.pq, T.ps, 128 * b, T.mq, T.ms, 128)
+            t_mm = [mm(arrived + [t_mo[c]], T.psc[:, 512 * c:512 * c + 128], 128 * c, T.pq, T.ps, M, T.mq, T.ms, 128)
                     for c in range(4)]
-            t_red = [None] * 4
             nb = B + 128
-            t_b4 = [None] * 4
-            for c in range(4):
-                i = 4 * b + c
-                m1, s1, out = T.mx[:, i:i + 1], T.srp[:, i:i + 1], T.bc[:, nb + 32 * c:nb + 32 * c + 32]
-                t_red[c] = rmax([t_mm[c]], m1, T.psc[:, 512 * c:512 * c + 128])
-                if c < 3:
-                    t_b4[c] = act([t_red[c], t_srp, t_quart], out, T.quart[:], AF.Identity, bias=s1, scale=m1)
-                else:
-                    t_b4[c] = ts([t_red[c]], out, T.quart[:], m1, s1, OP.mult, OP.add)
-            turn([t_b4[2]], T.srt[:, nb:nb + 96], T.bc[:, nb:nb + 96])
-            t_srt = turn([t_b4[3]], T.srt[:, nb + 96:nb + 128], T.bc[:, nb + 96:nb + 128])
-            t_m = t_red[3]
-            t_ext = [mm([t_red[c], t_eq], T.psc[:, 512 * c:512 * c + 128], 128 * c, T.eq, T.es, 128 * b, T.mq, T.ms, 128)
-                     for c in range(4)]
+            t_b4, t_m = [None] * 4, [None] * 4
+            for c in range(6):
+                if c < 4:
+                    X = 384 * b + 96 * c
+                    t_m[c] = scan([t_mm[c], t_mo[3]], T.mx[:, X:X + 96], T.psc[:, 512 * c + K:512 * c + 128], T.low[:],
+                                  T.mo[:, i + c:i + c + 1], OP.max, OP.max)
+                k = c if c < 2 else c - 2
+                X = 384 * b + 96 * k
+                m1, s1, out = T.mx[:, X + 95:X + 96], T.srp[:, i + k:i + k + 1], T.bc[:, nb + 32 * k:nb + 32 * k + 32]
+                if c < 2:
+                    t_b4[k] = act([t_m[k], t_srp], out, T.quart[:], AF.Identity, bias=s1, scale=m1)
+                elif c >= 4:
+                    t_b4[k] = ts([t_m[k]], out, T.quart[:], m1, s1, OP.mult, OP.add)
+            X = 384 * b
+            t_q = ts([], T.mq4[:, i:i + 4], T.mx[:, X + 95:X + 384:96], -0.25, None, OP.mult)
+            t_srt = [turn(t_b4[2 * h:2 * h + 2], T.srt[:, nb + 64 * h:nb + 64 * h + 64],
+                          T.bc[:, nb + 64 * h:nb + 64 * h + 64]) for h in range(2)]
+            t_st = tt([t_q], T.st[:, i + 4:i + 8] if b < R - 2 else T.sf[:, 0:4], T.mq4[:, i:i + 4], T.st[:, i:i + 4],
+                      OP.add)
         for o in range(O):
-            t_y[o] = mm(arrived + [t_wq] + ([free_y[o]] if free_y[o] else []), T.psy[:, 512 * o:512 * o + 128],
-                        128 * o, T.wq, T.ws, 128 * b, T.mq, T.ms, 128)
+            t_y[o] = mm(arrived + [t_wq] + ([free_y[o]] if free_y[o] else []), psy[o],
+                        128 * o, T.wq, T.ws, M, T.mq, T.ms, 128)
         if b == R - 1:
             store(b, 0, "V")
             store(b, 1, "S")

@@ -3,13 +3,13 @@ from concourse.mybir import dt, AluOpType, AxisListType, ActivationFunctionType
 
 OP = AluOpType
 P, K, R, O, N = 512, 32, 4, 2, 4
-PIECE = (0, 2, 1, 3)
+PIECE = (3, 2, 1, 0)
+UW = 256
 LW = 132
 KAPPA = 2.0 ** -24 * (1.0 + 2.0 ** -10)
 TINY = 2.0 ** -124
 LOW = -9e29
 GONE = -1e29
-STEP = 4096.0
 
 
 def _sbuf(dtype, **widths):
@@ -17,16 +17,17 @@ def _sbuf(dtype, **widths):
 
 
 SCRATCH = {
-    **_sbuf("bfloat16", uc=4, ones=128, ut=512, xr=4 * P, xp=4 * P, wr=512 * O, i32=32, i16=256, cmp=P * R, en=128 * R,
-            ent=128 * R, cm2=96 * R, r2=48 * R, hb=2 * R, ab=4 * LW, fl=32 * R, flt=32 * R),
-    **_sbuf("float8_e4m3fn_x4", xq=P, pq=P, wq=128 * O, mq=128 * (R + 1), abq=LW),
-    **_sbuf("uint8", xs=P, ps=P, ws=128 * O, ms=128 * (R + 1), abs=LW),
-    **_sbuf("float32", tri=32, quart=32, low=96, num=P, at=4, base=1, zero=2, bc=128 * R, srt=128 * R, th=128 * R,
-            dd=4 * R, rs=256 * R, ev=128 * R, evt=192, vs=96 * R, enj=128 * R, p4=R, gg=64 * R, chs=K * R, cnt=R,
-            pen=4 * R, srp=4 * R, mo=4 * R, mx=384 * R, mq4=4 * R, st=4 * R, sf=32, sft=32, ysb=O * P),
+    **_sbuf("bfloat16", uc=4, ones=128, ut=4 * UW, xr=4 * P, xp=4 * P, wr=512 * O, i32=32, i16=256, lim=32, cmp=P * R,
+            ne=128 * R, cm2=256 * R, sg=256 * R, bh=128, bl=128, pos=256 * R, ab=4 * LW, fl=32 * R, flt=32 * R),
+    **_sbuf("float8_e4m3fn_x4", xq=P, pq=P, wq=128 * O, mq=UW + 128 * R, abq=LW),
+    **_sbuf("uint8", xs=P, ps=P, ws=128 * O, ms=UW + 128 * R, abs=LW),
+    **_sbuf("float32", tri=32, quart=32, low=96, num=P, at=4, at2=1, zero=2, bc=128 * R, srt=128 * R,
+            th=128 * R, up=128 * R, upt=128 * R, dd=4 * R, rs=256 * R, ev=128 * R, evt=128 * R, vs=64 * R,
+            ro=384 * R, r2=128 * R, acc=R, chs=K * R, cnt=R, pen=4 * R, srp=4 * R, mo=4 * R, mx=384 * R,
+            mq4=4 * R, st=4 * R, sf=32, sft=32, ysb=O * P),
     **_sbuf("uint16", off=2 * R),
     "psc": ("psum", [128, 2048], "float32"),
-    "psr": ("psum", [128, 2048], "float32"),
+    "psr": ("psum", [128, 1536], "float32"),
 }
 SEMAPHORES = ["sv", "ss", "sp", "sg", "du", "dx0", "dx1", "dx2", "dx3", "dw", "dout",
               "arr0", "arr1", "arr2", "arr3", "loc"]
@@ -92,9 +93,13 @@ def rank_program(g, core, T, topo):
     def fill(ap, v):
         return done("V", g.vector.memset(ap, v))
 
-    def whole(out, pattern, step):
+    def whole(out, pattern, step, start=0):
         need("G", [("sg", count.get("sg", 0))])
-        return done("G", g.iota(out, pattern, 0, step, allow_small_or_imprecise_dtypes=True))
+        return done("G", g.iota(out, pattern, start, step, allow_small_or_imprecise_dtypes=True))
+
+    def spread(deps, out, in_, channels):
+        need("G", [("sg", count["sg"])] + list(deps))
+        return done("G", g.partition_broadcast(out, in_, channels))
 
     def quant(deps, q, s, a, n, src, sa):
         need("V", deps)
@@ -106,57 +111,54 @@ def rank_program(g, core, T, topo):
                                             rq[:, r:r + n], rs[:, r:r + n], start, stop))
 
     quad = [slice(32 * a, 32 * a + 32) for a in range(4)]
-    half = [slice(0, 64), slice(64, 128)]
 
     du = dma("Y", T.uc[:], T.u[:, 0:4], "du")
     dx = [None] * 4
     for a in range(4):
-        dx[a] = dma("SYSY"[a], T.xr[:, 512 * a:512 * a + 512], T.x[:, 512 * a:512 * a + 512], "dx%d" % a)
-    dw = dma("Y", T.wr[:], T.w[:], "dw", [dx[2], dx[3]])
+        j = PIECE[a]
+        dx[j] = dma("SYSY"[a], T.xr[:, 512 * j:512 * j + 512], T.x[:, 512 * j:512 * j + 512], "dx%d" % j)
+    dw = dma("Y", T.wr[:], T.w[:], "dw", dx)
 
     t_ones = fill(T.ones[:], 1.0)
-    fill(T.quart[:], -0.25)
-    fill(T.low[:], LOW)
-    fill(T.zero[:], 0.0)
-    fill(T.sf[:], 0.0)
-    fill(T.evt[:], 0.0)
-    fill(T.ab[:], 0.0)
-    for a in range(4):
-        fill(T.base[quad[a], :], 128.0 * PIECE[a] - STEP)
+    t_zero = fill(T.ut[:, 512:4 * UW], 0.0)
+    fill(T.ut[:, 0:384], 0.0)
+    for out, v in ((T.zero[:], 0.0), (T.ab[:, 512:4 * LW], 0.0), (T.lim[:], 2.0 * K - 128), (T.bh[:, 0:127], 0.0),
+                   (T.bl[:, 0:127], -1.0)):
+        act([t_ones], out, T.ones[:, 0:out.shape[1]], AF.Identity, scale=v)
+    quant([t_zero], T.mq, T.ms, 128, 128, T.ut, 512)
+    for t in range(2):
+        t_ut = ts([du], T.ut[:, 384 + t:512:4], T.ones[:, 0:32], T.uc[:, t:t + 1], None, OP.mult)
+        t_us = act([du], T.ut[:, 386 + t:512:4], T.ones[:, 0:32], AF.Identity, bias=T.uc[:, 2 + t:3 + t], scale=0.0)
     for a in range(4):
         whole(T.at[quad[a], :], [[32, 4]], 1)
     t_i32 = whole(T.i32[:], [[1, 32]], 0)
-    t_i16 = whole(T.i16[:], [[16, 2], [0, 8], [1, 16]], 0)
-    t_num = whole(T.num[:], [[1, P]], 0)
+    t_i16 = whole(T.i16[:], [[32, 2], [0, 8], [2, 16]], 0, -128)
 
-    for t in range(4):
-        t_ut = ts([du, t_ones], T.ut[:, t:512:4], T.ones[:], T.uc[:, t:t + 1], None, OP.mult)
-
-    def reorder(a):
+    def reorder(a, vector=False):
         j = PIECE[a]
         for c in range(4):
-            t = act([dx[j]], T.xp[:, 512 * c + 128 * a:512 * c + 128 * a + 128],
-                    T.xr[:, 512 * j + 128 * c:512 * j + 128 * c + 128], AF.Copy)
+            out = T.xp[:, 512 * c + 128 * a:512 * c + 128 * a + 128]
+            in_ = T.xr[:, 512 * j + 128 * c:512 * j + 128 * c + 128]
+            t = cp([], out, in_) if vector else act([dx[j]], out, in_, AF.Copy)
         return t
 
-    t_m = [None] * 4
+    reorder(0)
+    reorder(1)
     for a in range(4):
         j = PIECE[a]
         t_xq = quant([dx[j]], T.xq, T.xs, 128 * j, 128, T.xr, 512 * j)
         if a == 0:
-            t_uq = quant([t_ut], T.mq, T.ms, 0, 128, T.ut, 0)
-            reorder(0)
-        t_m[a] = mm([t_xq, t_uq], T.psc[:, 512 * a:512 * a + 128], 0, T.mq, T.ms, 128 * j, T.xq, T.xs, 128)
-        t_m2 = mm([], T.psr[:, 512 * a:512 * a + 128], 0, T.mq, T.ms, 128 * j, T.xq, T.xs, 128)
-        t_row = act([t_m2], T.srt[quad[a], 0:128], T.psr[quad[a], 512 * a:512 * a + 128], AF.Copy)
+            t_uq = quant([t_ut, t_us], T.mq, T.ms, 0, 128, T.ut, 0)
+        t_m = mm([t_uq, t_xq], T.psc[:, 0:128], 96 - 32 * a, T.mq, T.ms, 128 * j, T.xq, T.xs, 128, a == 0, a == 3)
     for a in range(4):
-        if a == 3:
-            t_tri = ts([t_i32], T.tri[:], T.i32[:], T.at[:, 0:1], None, OP.is_ge)
-        t_turn = turn([t_m[a]], T.bc[quad[a], 0:128], T.psc[quad[a], 512 * a:512 * a + 128])
-    t_b4 = [t_turn] * 4
-    t_srt = [t_row] * 2
+        fill(T.bh[quad[a], 127:128], 128.0 * PIECE[a] + 96)
+    t_tri = ts([t_i32], T.tri[:], T.i32[:], T.at[:, 0:1], None, OP.is_ge)
+    t_b4 = [turn([t_m], T.bc[:, 0:128], T.psc[:, 0:128])] * 4
+    t_srt = [cp([], T.srt[:, 0:128], T.psc[:, 0:128])] * 4
+    ts([], T.at2[:], T.at[:, 0:1], 2.0, None, OP.mult)
+    fill(T.bl[:, 127:128], 15.0)
 
-    dests = [c for c in T.cores if c != core]
+    dests = [T.cores[(rank + k) % N] for k in range(1, N)]
     mask = topo.mask(core, dests[0])
     ids = []
     for c in dests:
@@ -166,7 +168,7 @@ def rank_program(g, core, T, topo):
     engs = bin(mask).count("1")
 
     def place(b, sender, holder):
-        return 128 * (b + 1) + K * ((sender - holder) % N if b < R - 1 else sender)
+        return UW + 128 * b + K * ((sender - holder) % N if b < R - 1 else sender)
 
     def send(buf, b, codes):
         views = [buf[:, place(b, rank, T.rank_of(c)):place(b, rank, T.rank_of(c)) + K] for c in [core] + dests]
@@ -179,7 +181,7 @@ def rank_program(g, core, T, topo):
     t_y = [None] * O
     free_y = [None] * O
     outs = []
-    psy = [T.psr[:, 1024 + 512 * o:1024 + 512 * o + 128] for o in range(O)]
+    psy = [T.psr[:, 512 + 512 * o:512 + 512 * o + 128] for o in range(O)]
 
     def store(b, o, e):
         c0 = P * o + 128 * b
@@ -192,77 +194,96 @@ def rank_program(g, core, T, topo):
             outs.append(dma(q, T.y[:, c0:c0 + cut], T.ysb[:, c0 + 128 - cut:c0 + 128], "dout"))
 
     for b in range(R):
-        B = 128 * b
+        B, C, i, G, S, H = 128 * b, P * b, 4 * b, 384 * b, 256 * b, 64 * b
+        row = slice(B, B + 128)
+        blk = [slice(B + 32 * c, B + 32 * c + 32) for c in range(4)]
         sc = [T.bc[:, B + 32 * c:B + 32 * c + 1] for c in range(4)]
-        t_d = act(t_b4, T.dd[:, 4 * b:4 * b + 4], T.bc[:, B:B + 128:32], AF.Abs, bias=TINY, scale=KAPPA)
-        t_th = [act([t_d, t_tri], T.th[:, B + 32 * c:B + 32 * c + 32], T.tri[:], AF.Identity, bias=sc[c],
-                    scale=T.dd[:, 4 * b + c:4 * b + c + 1]) for c in range(4)]
+        dd = [T.dd[:, i + c:i + c + 1] for c in range(4)]
         if b:
-            for o in range(O):
-                store(b - 1, o, "S")
+            t_d = [act([t_b4[c]], dd[c], sc[c], AF.Abs, bias=TINY, scale=KAPPA) for c in range(4)]
         else:
-            reorder(1)
-            reorder(2)
-        C, i = P * b, 4 * b
-        for c, lo in ((1, 1), (2, 1), (0, 0), (1, 0), (2, 0), (3, 1)):
+            t_d = [act(t_b4, T.dd[:, 0:4], T.bc[:, 0:128:32], AF.Abs, bias=TINY, scale=KAPPA)] * 4
+        t_th = [act([t_tri, t_d[c]], T.th[:, blk[c]], T.tri[:], AF.Identity, bias=sc[c], scale=dd[c]) for c in range(4)]
+        for c in range(4):
+            t_up = act([], T.up[:, blk[c]], T.ones[:, 0:32], AF.Identity, bias=sc[c], scale=dd[c])
+        slot = [slice(G + 128 * k, G + 128 * k + 128) for k in range(3)]
+        t_pb = spread(t_srt, T.ro[:, slot[0]], T.srt[0:1, row], 128)
+        for a, k, src in ((2, 2, 1), (3, 2, 1), (3, 1, 2)):
+            t_x = act(t_srt, T.ro[quad[a], slot[k]], T.srt[quad[src], row], AF.Copy)
+        for c, lo in ((1, 1), (2, 1), (3, 1), (0, 0), (1, 0), (2, 0)):
             j0, j1 = (0, 32 * c) if lo else (32 * c + 32, 128)
-            ts([t_srt[int(j1 > 64)]] + t_b4, T.cmp[:, C + 128 * c + j0:C + 128 * c + j1], T.srt[:, B + j0:B + j1], sc[c],
+            ts([t_b4[c], t_srt[j1 // 32 - 1]], T.cmp[:, C + 128 * c + j0:C + 128 * c + j1], T.srt[:, B + j0:B + j1], sc[c],
                None, OP.is_ge if lo else OP.is_gt)
-        t_c = [tt([t_th[c]], T.cmp[:, C + 160 * c:C + 160 * c + 32], T.srt[:, B + 32 * c:B + 32 * c + 32],
-                  T.th[:, B + 32 * c:B + 32 * c + 32], OP.is_ge) for c in range(4)]
-        S = 256 * b
+        t_c = [tt([t_th[c]], T.cmp[:, C + 160 * c:C + 160 * c + 32], T.srt[:, blk[c]], T.th[:, blk[c]], OP.is_ge)
+               for c in range(4)]
         t_rs = [scan([t_c[c]], T.rs[:, S + 64 * c:S + 64 * c + 64], T.cmp[:, C + 128 * c:C + 128 * c + 64],
                      T.cmp[:, C + 128 * c + 64:C + 128 * c + 128], 0.0, OP.add, OP.add) for c in range(4)]
-        r1 = [T.rs[:, S + 64 * c + 63:S + 64 * c + 64] for c in range(4)]
-        t_ev = [ts([t_rs[c]], T.ev[:, B + 32 * c:B + 32 * c + 32], T.i32[:], r1[c], sc[c], OP.is_equal, OP.mult)
-                for c in range(4)]
-        for c in range(4):
-            t_en = ts([], T.en[:, B + 32 * c:B + 32 * c + 32], T.i32[:], r1[c], T.at[:, c:c + 1], OP.is_equal, OP.mult)
-        for h in range(2):
-            t_evt = turn([t_ev[2 * h + 1]], T.evt[:, 96 * h:96 * h + 64], T.ev[:, B + 64 * h:B + 64 * h + 64])
-        t_ent = turn([t_en], T.ent[:, B:B + 128], T.en[:, B:B + 128])
-        G, H = 96 * b, 64 * b
-        t_vs = scan([t_evt], T.vs[:, G:G + 96], T.evt[:, 0:96], T.evt[:, 96:192], 0.0, OP.add, OP.add)
-        p4, hb = T.p4[:, b:b + 1], T.hb[:, 2 * b:2 * b + 2]
-        t_p4 = act([t_ent], T.enj[:, B:B + 128], T.ent[:, B:B + 128], AF.Identity, bias=STEP / 128, accum_out=p4)
-        t_hb = act([t_p4], hb, T.zero[:], AF.Identity, bias=p4)
-        act([t_hb], T.ab[:, 512:518:5], hb, AF.Identity, bias=T.base[:])
-        t_lo = act([], T.ab[:, 520:526:5], hb, AF.Identity, bias=p4, scale=-1.0)
+        t_upt = turn([t_up], T.upt[:, row], T.up[:, row])
+        t_pb2 = spread([t_upt], T.ro[0:96, slot[1]], T.upt[96:97, row], 96)
         if b == 0:
-            t_xp = reorder(3)
-
-        t_g = [turn([t_vs], T.gg[:, H:H + 32], T.vs[:, G + 64:G + 96])]
-        t_g += [turn([], T.gg[half[h], H + 32:H + 64], T.vs[half[1 - h], G + 64:G + 96]) for h in range(2)]
+            t_num = whole(T.num[:], [[1, P]], 0)
+        for a, k, src in ((0, 0, 1), (0, 2, 2), (1, 2, 2)):
+            t_ro = act([t_pb, t_upt], T.ro[quad[a], slot[k]], T.upt[quad[src], row], AF.Copy)
+        t_ev = [ts([t_rs[c]], T.ev[:, blk[c]], T.i32[:], T.rs[:, S + 64 * c + 63:S + 64 * c + 64],
+                   T.up[:, B + 32 * c:B + 32 * c + 1], OP.is_equal, OP.mult) for c in range(4)]
+        if b:
+            X = 384 * (b - 1)
+            t_q = ts([], T.mq4[:, i:i + 4], T.mx[:, X + 95:X + 384:96], -0.25, None, OP.mult)
+        else:
+            fill(T.ab[:, 2:512:4], 0.0)
         for h in range(2):
-            ts(t_g[:1], T.cm2[half[h], G:G + 32], T.gg[half[1 - h], H:H + 32], T.vs[half[h], G + 95:G + 96], None,
-               OP.is_ge if h else OP.is_gt)
-        for a in range(4):
-            t_c2 = ts([t_g[1 + a // 2]], T.cm2[quad[a], G + 32:G + 96], T.gg[quad[a ^ 1], H:H + 64],
-                      T.vs[quad[a], G + 95:G + 96], None, OP.is_ge if a & 1 else OP.is_gt)
-        t_r2 = scan([t_c2], T.r2[:, 48 * b:48 * b + 48], T.cm2[:, G:G + 48], T.cm2[:, G + 48:G + 96], T.at[:, 0:1],
-                    OP.add, OP.add)
-        rk = T.r2[:, 48 * b + 47:48 * b + 48]
+            t_evt = turn([t_ev[2 * h + 1]], T.evt[:, B + 64 * h:B + 64 * h + 64], T.ev[:, B + 64 * h:B + 64 * h + 64])
+        if b:
+            store(b - 1, 0, "V")
+        else:
+            fill(T.bh[:, 31:96:32], -32.0)
+            fill(T.bl[:, 31:96:32], 31.0)
+        t_vs = scan([t_evt], T.vs[:, H:H + 64], T.evt[:, B:B + 64], T.evt[:, B + 64:B + 128], 0.0, OP.add, OP.add)
+        t_ne = ts([], T.ne[:, row], T.evt[:, row], 0.0, None, OP.is_equal)
+
+        v, acc = T.vs[:, H + 63:H + 64], T.acc[:, b:b + 1]
+        t_sg = act([t_ro, t_vs], T.sg[:, S:S + 128], T.ro[:, slot[2]], AF.Sign, bias=v, scale=-1.0)
+        t_acc = act([t_sg], T.sg[:, S + 128:S + 256], T.sg[:, S:S + 128], AF.Sign, bias=0.5, scale=-1.0, accum_out=acc)
+        for k in range(2):
+            t_c2 = ts([t_x, t_pb2] if k else [t_ro, t_vs], T.cm2[:, S + 128 * k:S + 128 * k + 128], T.ro[:, slot[k]], v,
+                      2.0, OP.is_ge, OP.mult)
+        for h, back in enumerate((T.bh, T.bl)):
+            t_p = scan([t_ne], T.pos[:, S + 128 * h:S + 128 * h + 128], T.ne[:, row], back[:], 0.0, OP.mult, OP.add)
+            t_lo = act([t_p], T.ab[:, 512 + 8 * h:518 + 8 * h:5], T.zero[:], AF.Identity,
+                       bias=T.pos[:, S + 128 * h + 127:S + 128 * h + 128])
+        if b:
+            store(b - 1, 1, "S")
+        else:
+            t_xp = reorder(2)
+        t_r2 = scan([t_c2], T.r2[:, row], T.cm2[:, S:S + 128], T.cm2[:, S + 128:S + 256], T.at2[:], OP.add, OP.add)
+        rk = T.r2[:, B + 127:B + 128]
+        if b:
+            t_st = tt([t_q], T.st[:, i:i + 4] if b < R - 1 else T.sf[:, 0:4], T.mq4[:, i:i + 4], T.st[:, i - 4:i], OP.add)
+        else:
+            fill(T.ab[:, 3:512:4], 0.0)
 
         for h in range(2):
-            t_a = ts([t_r2, t_i16], T.ab[:, h:512:4], T.i16[:, 128 * h:128 * h + 128], rk, None, OP.is_equal)
+            t_a = ts([t_i16, t_acc, t_r2], T.ab[:, h:512:4], T.i16[:, 128 * h:128 * h + 128], rk, acc, OP.subtract,
+                     OP.is_equal)
         if b < R - 1:
-            t_fl = ts([], T.fl[:, 32 * b:32 * b + 32], T.ones[:, 0:32], rk, float(K), OP.mult, OP.is_lt)
-        t_abq = quant([t_a, t_lo], T.abq, T.abs, 0, LW, T.ab, 0)
+            t_fl = ts([], T.fl[:, 32 * b:32 * b + 32], T.lim[:], rk, acc, OP.subtract, OP.is_gt)
+        else:
+            t_sft = turn([t_st], T.sft[:], T.sf[:])
+            for a in range(4):
+                j = 128 * PIECE[a]
+                outs.append(dma("Y", T.se[0:1, j:j + 128], T.sft[32 * a:32 * a + 4, :], "dout", [t_sft]))
+        t_abq = quant([t_lo, t_a], T.abq, T.abs, 0, LW, T.ab, 0)
         mm([t_abq], T.psr[:, 0:128], 0, T.abq, T.abs, 2, T.abq, T.abs, 128, True, False)
         t_l = mm([], T.psr[:, 0:128], 0, T.abq, T.abs, 4, T.abq, T.abs, 128, False, True)
         if b < R - 1:
             t_flt = turn([t_fl], T.flt[:, 32 * b:32 * b + 32], T.fl[:, 32 * b:32 * b + 32])
             if b == 0:
-                quant([t_xp], T.pq, T.ps, 0, 256, T.xp, 0)
+                t_xv = reorder(3, True)
             t_cnt = red([t_flt], T.cnt[:, b:b + 1], T.flt[:, 32 * b:32 * b + 32], OP.add)
-            if b == 0:
-                quant([], T.pq, T.ps, 256, 128, T.xp, 1024)
         off = T.off[:, 2 * b:2 * b + 2]
-        t_off = cp([t_l], off, T.psr[:, 126:128])
+        t_off = ts([t_l], off, T.psr[:, 126:128], 16.0, None, OP.add)
         if b < R - 1:
             t_pen = ts([t_cnt], T.pen[:, i:i + 4], T.rs[:, S + 63:S + 256:64], T.cnt[:, b:b + 1], GONE, OP.is_lt, OP.mult)
-        if b == 0:
-            t_pq = quant([], T.pq, T.ps, 384, 128, T.xp, 1536)
 
         m0 = place(b, rank, rank)
         t_pk = cp([t_off], T.mq[:, m0:m0 + K].bitcast(dt.uint32), T.xq[:, 0:P].bitcast(dt.uint32).indirect(off))
@@ -273,53 +294,44 @@ def rank_program(g, core, T, topo):
         send(T.ms, b, False)
 
         t_ch = act([t_num], T.chs[:, K * b:K * b + K], T.num[:, 0:P].indirect(off), AF.Copy)
+        if b == 0:
+            t_pq = [quant([t_xp, t_xv], T.pq, T.ps, 256 * h, 256, T.xp, 1024 * h) for h in range(2)]
         if b < R - 1:
-            t_own = [mm([t_pk, t_psc, t_pq], T.psc[:, 512 * c:512 * c + 128], 128 * c, T.pq, T.ps, m0 + K - 128,
+            t_own = [mm([t_pk, t_psc, t_pq[c // 2]], T.psc[:, 512 * c:512 * c + 128], 128 * c, T.pq, T.ps, m0 + K - 128,
                         T.mq, T.ms, 128) for c in range(4)]
             t_srp = tt([t_pen], T.srp[:, i:i + 4], T.bc[:, B:B + 128:32], T.pen[:, i:i + 4], OP.add)
             if b == 0:
                 t_st = cp([], T.st[:, 0:4], T.bc[:, 0:128:32])
-                t_wq = quant([dw], T.wq, T.ws, 0, 128 * O, T.wr, 0)
+                fill(T.quart[:], -0.25)
+                fill(T.low[:], LOW)
             t_mo = [red([t_own[c]], T.mo[:, i + c:i + c + 1], T.psc[:, 512 * c + 128 - K:512 * c + 128], OP.max)
                     for c in range(4)]
+            if b == 0:
+                t_wq = quant([dw], T.wq, T.ws, 0, 128 * O, T.wr, 0)
+                fill(T.sf[:], 0.0)
         else:
-            t_sft = turn([t_st], T.sft[:], T.sf[:])
             outs.append(dma("Y", T.ch[:], T.chs[0:1, :], "dout", [t_ch]))
-            for a in range(4):
-                j = 128 * PIECE[a]
-                outs.append(dma("Y", T.se[0:1, j:j + 128], T.sft[32 * a:32 * a + 4, :], "dout", [t_sft]))
 
-        arrived = [("arr%d" % b, (N - 1) * 2 * engs), t_pk, t_psc]
-        M = 128 * (b + 1)
+        arrived = [t_pk, t_psc, ("arr%d" % b, (N - 1) * 2 * engs)]
+        M = UW + 128 * b
         if b < R - 1:
-            t_mm = [mm(arrived + [t_mo[c]], T.psc[:, 512 * c:512 * c + 128], 128 * c, T.pq, T.ps, M, T.mq, T.ms, 128)
+            t_mm = [mm([t_mo[3]] + arrived, T.psc[:, 512 * c:512 * c + 128], 128 * c, T.pq, T.ps, M, T.mq, T.ms, 128)
                     for c in range(4)]
             nb = B + 128
-            t_b4, t_m = [None] * 4, [None] * 4
-            for c in range(6):
-                if c < 4:
-                    X = 384 * b + 96 * c
-                    t_m[c] = scan([t_mm[c], t_mo[3]], T.mx[:, X:X + 96], T.psc[:, 512 * c + K:512 * c + 128], T.low[:],
-                                  T.mo[:, i + c:i + c + 1], OP.max, OP.max)
-                k = c if c < 2 else c - 2
-                X = 384 * b + 96 * k
-                m1, s1, out = T.mx[:, X + 95:X + 96], T.srp[:, i + k:i + k + 1], T.bc[:, nb + 32 * k:nb + 32 * k + 32]
-                if c < 2:
-                    t_b4[k] = act([t_m[k], t_srp], out, T.quart[:], AF.Identity, bias=s1, scale=m1)
-                elif c >= 4:
-                    t_b4[k] = ts([t_m[k]], out, T.quart[:], m1, s1, OP.mult, OP.add)
-            X = 384 * b
-            t_q = ts([], T.mq4[:, i:i + 4], T.mx[:, X + 95:X + 384:96], -0.25, None, OP.mult)
-            t_srt = [turn(t_b4[2 * h:2 * h + 2], T.srt[:, nb + 64 * h:nb + 64 * h + 64],
-                          T.bc[:, nb + 64 * h:nb + 64 * h + 64]) for h in range(2)]
-            t_st = tt([t_q], T.st[:, i + 4:i + 8] if b < R - 2 else T.sf[:, 0:4], T.mq4[:, i:i + 4], T.st[:, i:i + 4],
-                      OP.add)
-        for o in range(O):
-            t_y[o] = mm(arrived + [t_wq] + ([free_y[o]] if free_y[o] else []), psy[o],
-                        128 * o, T.wq, T.ws, M, T.mq, T.ms, 128)
+            t_b4 = [None] * 4
+            for c in range(4):
+                X = 384 * b + 96 * c
+                t_m = scan([t_mo[3], t_mm[c]], T.mx[:, X:X + 96], T.psc[:, 512 * c + K:512 * c + 128], T.low[:],
+                           T.mo[:, i + c:i + c + 1], OP.max, OP.max)
+                t_b4[c] = act([t_m], T.bc[:, nb + 32 * c:nb + 32 * c + 32], T.quart[:], AF.Identity,
+                              bias=T.srp[:, i + c:i + c + 1], scale=T.mx[:, X + 95:X + 96])
+            t_srt = [turn([t_b4[c]], T.srt[:, nb + 32 * c:nb + 32 * c + 32], T.bc[:, nb + 32 * c:nb + 32 * c + 32])
+                     for c in range(4)]
+        for o in (1, 0):
+            t_y[o] = mm([t_wq] + [t for t in free_y if t] + arrived, psy[o], 128 * o, T.wq, T.ws, M, T.mq, T.ms, 128)
         if b == R - 1:
-            store(b, 0, "V")
             store(b, 1, "S")
+            store(b, 0, "V")
 
     need("Y", [outs[-1]])
     need("G", [("loc", 2 * R * engs)])

@@ -4,12 +4,14 @@ from concourse.mybir import dt, AluOpType, AxisListType, ActivationFunctionType
 OP = AluOpType
 P, K, R, O, N = 512, 32, 4, 2, 4
 PIECE = (3, 2, 1, 0)
-UW = 256
+UW = 128
 LW = 132
+FW = 262
+SCALAR = {0: 3, 1: 3, 2: 3, 3: 2}
 KAPPA = 2.0 ** -24 * (1.0 + 2.0 ** -10)
 TINY = 2.0 ** -124
-LOW = -9e29
-GONE = -1e29
+FLOOR = -2.0 ** 90
+GONE = 1e29
 
 
 def _sbuf(dtype, **widths):
@@ -18,19 +20,41 @@ def _sbuf(dtype, **widths):
 
 SCRATCH = {
     **_sbuf("bfloat16", uc=4, ones=128, ut=4 * UW, xr=4 * P, xp=4 * P, wr=512 * O, i32=32, i16=256, lim=32, cmp=P * R,
-            ne=128 * R, cm2=256 * R, sg=256 * R, bh=128, bl=128, pos=256 * R, ab=4 * LW, fl=32 * R, flt=32 * R),
-    **_sbuf("float8_e4m3fn_x4", xq=P, pq=P, wq=128 * O, mq=UW + 128 * R, abq=LW),
-    **_sbuf("uint8", xs=P, ps=P, ws=128 * O, ms=UW + 128 * R, abs=LW),
-    **_sbuf("float32", tri=32, quart=32, low=96, num=P, at=4, at2=1, zero=2, bc=128 * R, srt=128 * R,
-            th=128 * R, up=128 * R, upt=128 * R, dd=4 * R, rs=256 * R, ev=128 * R, evt=128 * R, vs=64 * R,
-            ro=384 * R, r2=128 * R, acc=R, chs=K * R, cnt=R, pen=4 * R, srp=4 * R, mo=4 * R, mx=384 * R,
-            mq4=4 * R, st=4 * R, sf=32, sft=32, ysb=O * P),
+            jp=128, tri=128, dg=P, sl=64 * R, ne=128 * R, cm2=256 * R, sg=256 * R, bh=128, bl=128, pos=256 * R,
+            ab=4 * LW, fl=32 * R, flt=32 * R, f0=4 * P, s0=256 * 4, r0=256 * 4, a0=4 * (FW + 32)),
+    **_sbuf("float8_e4m3fn_x4", xq=P, pq=P, wq=128 * O, mq=UW + 128 * R, abq=LW, q0=FW, fq=160),
+    **_sbuf("uint8", xs=P, ps=P, ws=128 * O, ms=UW + 128 * R, abs=LW, p0=FW, fs=160),
+    **_sbuf("float32", old=2 * P, strict=32, num=P, at=2, ei=4, epn=3, side=1, a32=1, zero=2,
+            sc=4, pr=8, srt=128 * R, th=128 * R, dd=4 * R, nz=4 * R, rs=256 * R, ev=128 * R, evt=128 * R,
+            vs=64 * R, r2=128 * R, ro=384 * R, acc=R, cl=R, c0=4, chs=K * R, cnt=R, pen=4 * R, mo=4 * R, mx=P * R,
+            st=4 * R, sf=32, sft=32, ysb=O * P),
     **_sbuf("uint16", off=2 * R),
     "psc": ("psum", [128, 2048], "float32"),
-    "psr": ("psum", [128, 1536], "float32"),
+    "psr": ("psum", [128, 2048], "float32"),
 }
-SEMAPHORES = ["sv", "ss", "sp", "sg", "du", "dx0", "dx1", "dx2", "dx3", "dw", "dout",
+SEMAPHORES = ["sv", "ss", "sp", "sg", "du", "dx0", "dx1", "dx2", "dx3", "dp0", "dp1", "dw", "dout",
               "arr0", "arr1", "arr2", "arr3", "loc"]
+
+FIRST = {
+    "V": "ones old bh0 bh1 bh2 bh3 blz sf tri xq0 ut0 ut1 ut2 uq xq1 xq2 xq3 a32 u10 strict tt0 u01 tt1 u20 u02 u12 "
+         "u21 u30 u31 tt2 rs0 tt3 rs1 a00 rs2 a01 rs3 a10 a11 a20 a21 a30 a31 "
+         "pen t0 abq abf t1 bhs bls off0 off1 ab2 pick pq0 pq1 wq mo0 mo1 mo2 mo3 ab3",
+    "S": "dx0 dx2 zero abz lim bh bl side epn ut3 az hold sc0 sc1 dg0 dg1 sc2 sc3 dg2 sg0 sg1 sg2 dg3 acc0 sg3 "
+         "acc1 acc2 acc3 lo hi tr00 tr10 tr20 tr30 tr01 tr11 tr21 tr31 psc ch tr02 tr12 tr22 tr32 tr03 tr13 tr23 tr33",
+    "P": "col0 col1 dup0 dup1 row0 row1 col2 col3 dup2 dup3 row2 l0 l1 fm0 fm1 fm2 fm3 own0 own1 own2 own3",
+    "G": "jp ei at0 at1 at2 at3 i32 i16 num sq ss",
+    "Y": "du dx1 dx3 re00 re10 re20 re30 re01 re11 re21 re31 re02 re12 re22 re32 re03 re13 re23 re33 dw",
+}
+LATER = {
+    "V": "mx0 mx1 mx2 mx3 turn0 turn1 turn2 turn3 lo2 lo3 tt0 hi0 tt1 hi1 hi2 tt2 tt3 rs0 rs1 rs2 rs3 "
+         "ev0 ev1 ev2 ev3 evt0 st evt1 yc1 vs ne sq4 c20 c21 pos0 pos1 sft r2 a0 a1 fl abq flt off0 off1 cnt pick "
+         "pen srp mo0 mo1 mo2 mo3",
+    "S": "dd0 dd1 dd2 th0 dd3 th1 sl th2 th3 lo1 nz ro0 ro1 ro2 ro3 ro4 ro5 yc0 sg acc b0 b1 psc ch",
+    "P": "mm0 mm1 mm2 mm3 ym1 ym0 l0 own0 own1 own2 own3",
+    "G": "pb0 pb1 sq ss",
+    "Y": "yd0 ye0 yd1 ye1 se0 se1 se2 se3",
+}
+LAST = {"V": "yc0", "S": "yc1 yd1", "P": "ym1 ym0", "G": "", "Y": "dch yd0"}
 
 
 def rank_program(g, core, T, topo):
@@ -40,123 +64,151 @@ def rank_program(g, core, T, topo):
     AF = ActivationFunctionType
     queue = {"V": g.vector, "S": g.scalar, "P": g.tensor, "G": g, "Y": g.sync}
     own = {"V": "sv", "S": "ss", "P": "sp", "G": "sg"}
-    count, seen = {}, {}
+    V, calls, now = g.vector, {}, [0]
 
-    def need(e, deps):
-        for s, v in deps:
-            if seen.get((e, s), 0) < v:
-                queue[e].wait_ge(T.sem[s], v)
-                seen[(e, s)] = v
+    def call(name, e, needs, issue, sem=None, n=1):
+        keys = []
+        for w in needs.split():
+            keys.append((w[:-1], now[0] - 1) if w[-1] == "-" else (w[:-1], 0) if w[-1] == "!" else (w, now[0]))
+        calls[(name, now[0])] = (e, keys, issue, sem or own[e], n)
 
-    def done(e, ins):
-        s = own[e]
-        count[s] = count.get(s, 0) + 1
-        ins.then_inc(T.sem[s], 1)
-        return (s, count[s])
+    def dma(name, e, needs, out, in_, sem):
+        call(name, e, needs, lambda: queue[e].dma_start(out, in_), sem, 16)
 
-    def dma(e, out, in_, sem, deps=()):
-        need(e, deps)
-        count[sem] = count.get(sem, 0) + 16
-        queue[e].dma_start(out, in_).then_inc(T.sem[sem], 16)
-        return (sem, count[sem])
+    def ts(name, needs, out, in0, s1, s2, *ops):
+        call(name, "V", needs, lambda: V.tensor_scalar(out, in0, s1, s2, *ops))
 
-    def ts(deps, out, in0, s1, s2, op0, op1=None):
-        need("V", deps)
-        if op1 is None:
-            return done("V", g.vector.tensor_scalar(out, in0, s1, s2, op0))
-        return done("V", g.vector.tensor_scalar(out, in0, s1, s2, op0, op1))
+    def tt(name, needs, out, in0, in1, op):
+        call(name, "V", needs, lambda: V.tensor_tensor(out, in0, in1, op))
 
-    def tt(deps, out, in0, in1, op):
-        need("V", deps)
-        return done("V", g.vector.tensor_tensor(out, in0, in1, op))
+    def cp(name, needs, out, in_):
+        call(name, "V", needs, lambda: V.tensor_copy(out, in_))
 
-    def cp(deps, out, in_):
-        need("V", deps)
-        return done("V", g.vector.tensor_copy(out, in_))
+    def turn(name, needs, out, in_):
+        call(name, "V", needs, lambda: V.transpose(out, in_))
 
-    def turn(deps, out, in_):
-        need("V", deps)
-        return done("V", g.vector.transpose(out, in_))
+    def scan(name, needs, out, d0, d1, init, op0, op1):
+        call(name, "V", needs, lambda: V.tensor_tensor_scan(out, d0, d1, init, op0, op1))
 
-    def scan(deps, out, d0, d1, init, op0, op1):
-        need("V", deps)
-        return done("V", g.vector.tensor_tensor_scan(out, d0, d1, init, op0, op1))
+    def red(name, needs, out, in_, op):
+        call(name, "V", needs, lambda: V.tensor_reduce(out, in_, AxisListType.X, op))
 
-    def red(deps, out, in_, op):
-        need("V", deps)
-        return done("V", g.vector.tensor_reduce(out, in_, AxisListType.X, op))
+    def act(name, needs, out, in_, func, **kw):
+        call(name, "S", needs, lambda: g.scalar.activation(out, in_, func, **kw))
 
-    def act(deps, out, in_, func, **kw):
-        need("S", deps)
-        return done("S", g.scalar.activation(out, in_, func, **kw))
+    def fill(name, ap, v, needs=""):
+        call(name, "V", needs, lambda: V.memset(ap, v))
 
-    def fill(ap, v):
-        return done("V", g.vector.memset(ap, v))
+    def whole(name, out, pattern, step, start=0):
+        call(name, "G", "", lambda: g.iota(out, pattern, start, step, allow_small_or_imprecise_dtypes=True))
 
-    def whole(out, pattern, step, start=0):
-        need("G", [("sg", count.get("sg", 0))])
-        return done("G", g.iota(out, pattern, start, step, allow_small_or_imprecise_dtypes=True))
+    def spread(name, needs, out, in_, channels):
+        call(name, "G", needs, lambda: g.partition_broadcast(out, in_, channels))
 
-    def spread(deps, out, in_, channels):
-        need("G", [("sg", count["sg"])] + list(deps))
-        return done("G", g.partition_broadcast(out, in_, channels))
+    def quant(name, needs, q, s, a, n, src, sa):
+        call(name, "V", needs, lambda: V.quantize_mx(q[:, a:a + n], s[:, a:a + n], src[:, sa:sa + 4 * n]))
 
-    def quant(deps, q, s, a, n, src, sa):
-        need("V", deps)
-        return done("V", g.vector.quantize_mx(q[:, a:a + n], s[:, a:a + n], src[:, sa:sa + 4 * n]))
-
-    def mm(deps, out, l, lq, ls, r, rq, rs, n, start=True, stop=True):
-        need("P", deps)
-        return done("P", g.tensor.matmul_mx(out, lq[:, l:l + 128], ls[:, l:l + 128],
-                                            rq[:, r:r + n], rs[:, r:r + n], start, stop))
+    def mm(name, needs, out, l, lq, ls, r, rq, rs, start=True, stop=True):
+        n = out.shape[1]
+        call(name, "P", needs, lambda: g.tensor.matmul_mx(out, lq[:, l:l + 128], ls[:, l:l + 128],
+                                                          rq[:, r:r + n], rs[:, r:r + n], start, stop))
 
     quad = [slice(32 * a, 32 * a + 32) for a in range(4)]
 
-    du = dma("Y", T.uc[:], T.u[:, 0:4], "du")
-    dx = [None] * 4
+    dma("du", "Y", "", T.uc[:], T.u[:, 0:4], "du")
+    for j in range(4):
+        dma("dx%d" % j, "SYSY"[j], "", T.xr[:, 512 * j:512 * j + 512], T.x[:, 512 * j:512 * j + 512], "dx%d" % j)
     for a in range(4):
-        j = PIECE[a]
-        dx[j] = dma("SYSY"[a], T.xr[:, 512 * j:512 * j + 512], T.x[:, 512 * j:512 * j + 512], "dx%d" % j)
-    dw = dma("Y", T.wr[:], T.w[:], "dw", dx)
-
-    t_ones = fill(T.ones[:], 1.0)
-    t_zero = fill(T.ut[:, 512:4 * UW], 0.0)
-    fill(T.ut[:, 0:384], 0.0)
-    for out, v in ((T.zero[:], 0.0), (T.ab[:, 512:4 * LW], 0.0), (T.lim[:], 2.0 * K - 128), (T.bh[:, 0:127], 0.0),
-                   (T.bl[:, 0:127], -1.0)):
-        act([t_ones], out, T.ones[:, 0:out.shape[1]], AF.Identity, scale=v)
-    quant([t_zero], T.mq, T.ms, 128, 128, T.ut, 512)
-    for t in range(2):
-        t_ut = ts([du], T.ut[:, 384 + t:512:4], T.ones[:, 0:32], T.uc[:, t:t + 1], None, OP.mult)
-        t_us = act([du], T.ut[:, 386 + t:512:4], T.ones[:, 0:32], AF.Identity, bias=T.uc[:, 2 + t:3 + t], scale=0.0)
-    for a in range(4):
-        whole(T.at[quad[a], :], [[32, 4]], 1)
-    t_i32 = whole(T.i32[:], [[1, 32]], 0)
-    t_i16 = whole(T.i16[:], [[32, 2], [0, 8], [2, 16]], 0, -128)
-
-    def reorder(a, vector=False):
-        j = PIECE[a]
         for c in range(4):
-            out = T.xp[:, 512 * c + 128 * a:512 * c + 128 * a + 128]
-            in_ = T.xr[:, 512 * j + 128 * c:512 * j + 128 * c + 128]
-            t = cp([], out, in_) if vector else act([dx[j]], out, in_, AF.Copy)
-        return t
+            j = 512 * PIECE[a] + 128 * c
+            dma("re%d%d" % (a, c), "Y", "dx0 dx1 dx2 dx3", T.xp[:, 512 * c + 128 * a:512 * c + 128 * a + 128],
+                T.x[:, j:j + 128], "dp%d" % (c // 2))
+    dma("dw", "Y", "", T.wr[:], T.w[:], "dw")
+    for h in range(2):
+        quant("pq%d" % h, " ".join("re%d%d" % (a, c) for a in range(4) for c in (2 * h, 2 * h + 1)),
+              T.pq, T.ps, 256 * h, 256, T.xp, 1024 * h)
+    quant("wq", "dw", T.wq, T.ws, 0, 128 * O, T.wr, 0)
 
-    reorder(0)
-    reorder(1)
+    fill("ones", T.ones[:], 1.0)
+    for t in range(3):
+        ts("ut%d" % t, "du ones", T.ut[:, t:512:4], T.ones[:], T.uc[:, t:t + 1], None, OP.mult)
+    act("ut3", "du ones", T.ut[:, 3:512:4], T.ones[:], AF.Identity, bias=T.uc[:, 3:4], scale=0.0)
+    quant("uq", "ut0 ut1 ut2 ut3", T.mq, T.ms, 0, 128, T.ut, 0)
+
+    for name, out, v in (("zero", T.zero[:], 0.0), ("abz", T.ab[:, 512:4 * LW], 0.0),
+                         ("az", T.a0[:, 1024:4 * FW], 0.0), ("hold", T.a0[:, 4 * FW:4 * FW + 128], FLOOR),
+                         ("lim", T.lim[:], float(K)), ("bh", T.bh[:, 0:127], 0.0), ("bl", T.bl[:, 0:127], -1.0)):
+        act(name, "ones", out, T.ones[:, 0:out.shape[1]], AF.Identity, scale=v)
     for a in range(4):
-        j = PIECE[a]
-        t_xq = quant([dx[j]], T.xq, T.xs, 128 * j, 128, T.xr, 512 * j)
-        if a == 0:
-            t_uq = quant([t_ut, t_us], T.mq, T.ms, 0, 128, T.ut, 0)
-        t_m = mm([t_uq, t_xq], T.psc[:, 0:128], 96 - 32 * a, T.mq, T.ms, 128 * j, T.xq, T.xs, 128, a == 0, a == 3)
+        whole("at%d" % a, T.at[quad[a], :], [[128 * (a // 2), 2]], 1)
+        fill("bh%d" % a, T.bh[quad[a], 127:128], 128.0 * PIECE[a] + 96)
+    whole("i32", T.i32[:], [[1, 32]], 0)
+    whole("i16", T.i16[:], [[16, 2], [0, 8], [1, 16]], 0)
+    whole("ei", T.ei[:], [[-32, 4]], 1)
+    whole("num", T.num[:], [[1, P]], 0)
+    fill("blz", T.bl[:, 127:128], 15.0)
+    fill("bhs", T.bh[:, 31:96:32], -32.0, "bh")
+    fill("bls", T.bl[:, 31:96:32], 31.0, "bl")
+    for t in (2, 3):
+        fill("ab%d" % t, T.ab[:, t:512:4], 0.0)
+    fill("old", T.old[:, 0:P], 0.0)
+    fill("sf", T.sf[:], 0.0)
+    whole("jp", T.jp[:], [[1, 128]], -1)
+    ts("tri", "jp", T.tri[:], T.jp[:], 0.0, TINY, OP.is_lt, OP.mult)
+    ts("strict", "i32 at3", T.strict[:], T.i32[:], T.at[:, 0:1], -1.0, OP.is_ge, OP.mult)
+    act("side", "ei", T.side[:], T.ei[:, 2:3], AF.Sign, bias=-0.5, scale=-1.0)
+    act("epn", "ei", T.epn[:], T.ei[:, 1:4], AF.Identity, bias=-2 * TINY, scale=-4 * TINY)
+    ts("a32", "ei at3", T.a32[:], T.ei[:, 0:1], T.at[:, 0:1], None, OP.subtract)
+    act("hi", "az i32 a32", T.a0[:, 1032:1036], T.i32[:, 0:4], AF.Identity, bias=T.a32[:], scale=128.0)
+    act("lo", "az at3", T.a0[:, 1036:1040], T.ones[:, 0:4], AF.Identity, bias=T.at[:, 0:1], scale=-16.0)
+
+    rows0 = [T.psc[:, 512 * j:512 * j + 128] for j in range(4)]
+    for c in range(4):
+        E, z = 512 * c, 512 * (c % 2)
+        twin = T.psr[:, 1024 + z:1152 + z]
+        quant("xq%d" % c, "dx%d" % c, T.xq, T.xs, 128 * c, 128, T.xr, 512 * c)
+        mm("col%d" % c, "uq xq%d" % c + " sc%d" % (c - 2) * (c > 1), T.psr[:, z:z + 128], 128 * c, T.xq, T.xs,
+           0, T.mq, T.ms)
+        if c < 3:
+            mm("row%d" % c, "uq xq%d" % c, rows0[c], 0, T.mq, T.ms, 128 * c, T.xq, T.xs)
+        mm("dup%d" % c, "uq xq%d" % c + " dg%d" % (c - 2) * (c > 1), twin, 0, T.mq, T.ms, 128 * c, T.xq, T.xs)
+        sc = T.sc[:, c:c + 1]
+        act("sc%d" % c, "col%d" % c, sc, T.psr[:, z:z + 1], AF.Copy)
+        act("dg%d" % c, "sc%d dup%d" % (c, c), T.dg[:, 128 * c:128 * c + 128], twin, AF.Identity, bias=sc, scale=-1.0)
+        tt("tt%d" % c, "tri dg%d" % c, T.f0[:, E:E + 128], T.dg[:, 128 * c:128 * c + 128], T.tri[:], OP.is_lt)
+        n, needs = 128, "tt%d" % c
+        for j in range(4):
+            if j == SCALAR.get(c):
+                sign, count = T.s0[:, 256 * c:256 * c + 128], T.s0[:, 256 * c + 128:256 * c + 256]
+                act("sg%d" % c, "sc%d dup%d" % (c, j), sign, T.psr[:, 512 * j:512 * j + 128], AF.Sign, bias=sc, scale=-1.0)
+                act("acc%d" % c, "sg%d" % c, count, sign, AF.Sign if j < c else AF.Relu, bias=float(j < c), scale=-1.0,
+                    accum_out=T.c0[:, c:c + 1])
+                needs += " acc%d" % c
+            elif j != c:
+                ts("u%d%d" % (c, j), "sc%d row%d" % (c, j), T.f0[:, E + n:E + n + 128], rows0[j], sc, None,
+                   OP.is_ge if j < c else OP.is_gt)
+                n, needs = n + 128, needs + " u%d%d" % (c, j)
+        end = 256 * c + 256
+        scan("rs%d" % c, needs, T.r0[:, end - n // 2:end], T.f0[:, E:E + n // 2], T.f0[:, E + n // 2:E + n],
+             T.c0[:, c:c + 1] if c in SCALAR else 0.0, OP.add, OP.add)
+        for h in range(2):
+            ts("a%d%d" % (c, h), "i16 rs%d" % c, T.a0[:, 512 * h + c:512 * h + 512:4], T.i16[:, 128 * h:128 * h + 128],
+               T.r0[:, end - 1:end], None, OP.is_equal)
+        mm("fm%d" % c, "abf abq", T.psc[:, 512 * c:512 * c + 160], 0, T.q0, T.p0, 0, T.fq, T.fs)
+    every = " ".join("a%d%d" % (c, h) for c in range(4) for h in range(2))
+    quant("abq", every + " hi lo", T.q0, T.p0, 0, FW, T.a0, 0)
+    quant("abf", every + " hi lo hold", T.fq, T.fs, 0, 160, T.a0, 4 * (FW - 128))
+    for h in range(2):
+        mm("l%d" % h, "abq", T.psr[:, 0:128], 128 * h, T.q0, T.p0, FW - 128 - 2 * h, T.q0, T.p0, h == 0, h == 1)
+        ts("off%d" % h, "l1", T.off[:, h:h + 1], T.psr[:, 124 + 2 * h:125 + 2 * h], T.psr[:, 125 + 2 * h:126 + 2 * h], 16.0,
+           OP.add, OP.add)
+    ts("pen", "rs0 rs1 rs2 rs3", T.pen[:, 0:4], T.r0[:, 255:1024:256], float(K), GONE, OP.is_lt, OP.mult)
+    ts("t0", "sc0 sc1 sc2 sc3", T.pr[:, 1:8:2], T.sc[:], -4.0, None, OP.mult)
+    tt("t1", "pen t0", T.pr[:, 0:8:2], T.pr[:, 1:8:2], T.pen[:, 0:4], OP.add)
     for a in range(4):
-        fill(T.bh[quad[a], 127:128], 128.0 * PIECE[a] + 96)
-    t_tri = ts([t_i32], T.tri[:], T.i32[:], T.at[:, 0:1], None, OP.is_ge)
-    t_b4 = [turn([t_m], T.bc[:, 0:128], T.psc[:, 0:128])] * 4
-    t_srt = [cp([], T.srt[:, 0:128], T.psc[:, 0:128])] * 4
-    ts([], T.at2[:], T.at[:, 0:1], 2.0, None, OP.mult)
-    fill(T.bl[:, 127:128], 15.0)
+        for c in range(4):
+            act("tr%d%d" % (a, c), "t1 old", T.old[quad[a], 128 * c + 96:128 * c + 96 + P + 1:P],
+                T.pr[quad[c], 2 * PIECE[a]:2 * PIECE[a] + 2], AF.Copy)
 
     dests = [T.cores[(rank + k) % N] for k in range(1, N)]
     mask = topo.mask(core, dests[0])
@@ -166,174 +218,171 @@ def rank_program(g, core, T, topo):
         rid, pid, _ = topo.addr(c)
         ids.append(DstId(rid=rid, pnc=pid))
     engs = bin(mask).count("1")
+    usable = [e for e in topo.engines(core, dests[0]) if mask >> e & 1]
+    halves = [sum(1 << e for e in usable[k::2]) for k in range(2)]
 
     def place(b, sender, holder):
         return UW + 128 * b + K * ((sender - holder) % N if b < R - 1 else sender)
 
-    def send(buf, b, codes):
+    def send(name, needs, buf, b, codes):
         views = [buf[:, place(b, rank, T.rank_of(c)):place(b, rank, T.rank_of(c)) + K] for c in [core] + dests]
         if codes:
             views = [v.bitcast(dt.uint8) for v in views]
-        g.remote_dma_fused([RemoteDMATransfer(dst_ids=ids, dma_engine_mask=mask, remote_sem=T.sem["arr%d" % b],
-                                              srcs=views[:1], dsts=views[1:])], local_sem=T.sem.loc)
+        m = halves[0 if codes else 1] if b == 0 else mask
+        call(name, "G", needs, lambda: g.remote_dma_fused(
+            [RemoteDMATransfer(dst_ids=ids, dma_engine_mask=m, remote_sem=T.sem["arr%d" % b], srcs=views[:1],
+                               dsts=views[1:])], local_sem=T.sem.loc), "loc", bin(m).count("1"))
 
-    t_wq = t_st = None
-    t_y = [None] * O
-    free_y = [None] * O
-    outs = []
     psy = [T.psr[:, 512 + 512 * o:512 + 512 * o + 128] for o in range(O)]
 
-    def store(b, o, e):
-        c0 = P * o + 128 * b
-        out = T.ysb[:, c0:c0 + 128]
-        free_y[o] = cp([t_y[o]], out, psy[o]) if e == "V" else act([t_y[o]], out, psy[o], AF.Copy)
-        cut = K * rank if b < R - 1 else 0
-        q = "Y" if b < R - 1 or o == 0 else "S"
-        outs.append(dma(q, T.y[:, c0 + cut:c0 + 128], T.ysb[:, c0:c0 + 128 - cut], "dout", [free_y[o]]))
-        if cut:
-            outs.append(dma(q, T.y[:, c0:c0 + cut], T.ysb[:, c0 + 128 - cut:c0 + 128], "dout"))
-
-    for b in range(R):
+    for b in range(R + 1):
+        now[0] = b
         B, C, i, G, S, H = 128 * b, P * b, 4 * b, 384 * b, 256 * b, 64 * b
         row = slice(B, B + 128)
         blk = [slice(B + 32 * c, B + 32 * c + 32) for c in range(4)]
-        sc = [T.bc[:, B + 32 * c:B + 32 * c + 1] for c in range(4)]
-        dd = [T.dd[:, i + c:i + c + 1] for c in range(4)]
         if b:
-            t_d = [act([t_b4[c]], dd[c], sc[c], AF.Abs, bias=TINY, scale=KAPPA) for c in range(4)]
-        else:
-            t_d = [act(t_b4, T.dd[:, 0:4], T.bc[:, 0:128:32], AF.Abs, bias=TINY, scale=KAPPA)] * 4
-        t_th = [act([t_tri, t_d[c]], T.th[:, blk[c]], T.tri[:], AF.Identity, bias=sc[c], scale=dd[c]) for c in range(4)]
-        for c in range(4):
-            t_up = act([], T.up[:, blk[c]], T.ones[:, 0:32], AF.Identity, bias=sc[c], scale=dd[c])
-        slot = [slice(G + 128 * k, G + 128 * k + 128) for k in range(3)]
-        t_pb = spread(t_srt, T.ro[:, slot[0]], T.srt[0:1, row], 128)
-        for a, k, src in ((2, 2, 1), (3, 2, 1), (3, 1, 2)):
-            t_x = act(t_srt, T.ro[quad[a], slot[k]], T.srt[quad[src], row], AF.Copy)
-        for c, lo in ((1, 1), (2, 1), (3, 1), (0, 0), (1, 0), (2, 0)):
-            j0, j1 = (0, 32 * c) if lo else (32 * c + 32, 128)
-            ts([t_b4[c], t_srt[j1 // 32 - 1]], T.cmp[:, C + 128 * c + j0:C + 128 * c + j1], T.srt[:, B + j0:B + j1], sc[c],
-               None, OP.is_ge if lo else OP.is_gt)
-        t_c = [tt([t_th[c]], T.cmp[:, C + 160 * c:C + 160 * c + 32], T.srt[:, blk[c]], T.th[:, blk[c]], OP.is_ge)
-               for c in range(4)]
-        t_rs = [scan([t_c[c]], T.rs[:, S + 64 * c:S + 64 * c + 64], T.cmp[:, C + 128 * c:C + 128 * c + 64],
-                     T.cmp[:, C + 128 * c + 64:C + 128 * c + 128], 0.0, OP.add, OP.add) for c in range(4)]
-        t_upt = turn([t_up], T.upt[:, row], T.up[:, row])
-        t_pb2 = spread([t_upt], T.ro[0:96, slot[1]], T.upt[96:97, row], 96)
-        if b == 0:
-            t_num = whole(T.num[:], [[1, P]], 0)
-        for a, k, src in ((0, 0, 1), (0, 2, 2), (1, 2, 2)):
-            t_ro = act([t_pb, t_upt], T.ro[quad[a], slot[k]], T.upt[quad[src], row], AF.Copy)
-        t_ev = [ts([t_rs[c]], T.ev[:, blk[c]], T.i32[:], T.rs[:, S + 64 * c + 63:S + 64 * c + 64],
-                   T.up[:, B + 32 * c:B + 32 * c + 1], OP.is_equal, OP.mult) for c in range(4)]
-        if b:
-            X = 384 * (b - 1)
-            t_q = ts([], T.mq4[:, i:i + 4], T.mx[:, X + 95:X + 384:96], -0.25, None, OP.mult)
-        else:
-            fill(T.ab[:, 2:512:4], 0.0)
-        for h in range(2):
-            t_evt = turn([t_ev[2 * h + 1]], T.evt[:, B + 64 * h:B + 64 * h + 64], T.ev[:, B + 64 * h:B + 64 * h + 64])
-        if b:
-            store(b - 1, 0, "V")
-        else:
-            fill(T.bh[:, 31:96:32], -32.0)
-            fill(T.bl[:, 31:96:32], 31.0)
-        t_vs = scan([t_evt], T.vs[:, H:H + 64], T.evt[:, B:B + 64], T.evt[:, B + 64:B + 128], 0.0, OP.add, OP.add)
-        t_ne = ts([], T.ne[:, row], T.evt[:, row], 0.0, None, OP.is_equal)
+            calls[("arr", b)] = (None, [], None, "arr%d" % (b - 1), (N - 1) * (2 if b > 1 else 1) * engs)
+            M = UW + B - 128
+            for o in range(O):
+                mm("ym%d" % o, "arr pick- psc- wq!" + (" yc%d-" % o if b > 1 else ""), psy[o], 128 * o, T.wq, T.ws,
+                   M, T.mq, T.ms)
+                c0 = P * o + B - 128
+                out = T.ysb[:, c0:c0 + 128]
+                if "yc%d" % o in (LATER if b < R else LAST)["V"]:
+                    cp("yc%d" % o, "ym%d" % o, out, psy[o])
+                else:
+                    act("yc%d" % o, "ym%d" % o, out, psy[o], AF.Copy)
+                cut = K * rank if b < R else 0
+                e = "Y" if b < R or o == 0 else "S"
+                dma("yd%d" % o, e, "yc%d" % o, T.y[:, c0 + cut:c0 + 128], T.ysb[:, c0:c0 + 128 - cut], "dout")
+                if cut:
+                    dma("ye%d" % o, e, "yc%d" % o, T.y[:, c0:c0 + cut], T.ysb[:, c0 + 128 - cut:c0 + 128], "dout")
+            if b == R:
+                dma("dch", "Y", "arr ch-", T.ch[:], T.chs[0:1, :], "dout")
+                break
+            for c in range(4):
+                X = C + 128 * c
+                placed = "srp-" if b > 1 else " ".join("tr%d%d-" % (a, c) for a in range(4))
+                mm("mm%d" % c, "arr mo%d-" % c, T.psc[:, 512 * c:512 * c + 128], 128 * c, T.pq, T.ps, M, T.mq, T.ms)
+                scan("mx%d" % c, "mm%d " % c + placed, T.mx[:, X:X + 128], T.psc[:, 512 * c + K:512 * c + 160],
+                     T.old[:, 128 * c:128 * c + 128], T.mo[:, i - 4 + c:i - 3 + c], OP.max, OP.add)
+                act("dd%d" % c, "mx%d" % c, T.dd[:, i + c:i + c + 1], T.mx[:, X + 96:X + 97], AF.Abs, bias=TINY,
+                    scale=KAPPA)
+                turn("turn%d" % c, "mx%d" % c, T.srt[:, blk[c]], T.mx[:, X + 96:X + 128])
+            ranked = T.mx[:, C + 96:C + P:128]
+            act("nz", "mx0 mx1 mx2 mx3", T.nz[:, i:i + 4], ranked, AF.Identity, bias=TINY)
+            tt("st", "mx0 mx1 mx2 mx3" + " st-" * (b > 1), T.st[:, i:i + 4], T.mx[:, C + 95:C + P:128],
+               T.st[:, i - 4:i] if b > 1 else T.old[:, P + 96:2 * P:128], OP.add)
 
-        v, acc = T.vs[:, H + 63:H + 64], T.acc[:, b:b + 1]
-        t_sg = act([t_ro, t_vs], T.sg[:, S:S + 128], T.ro[:, slot[2]], AF.Sign, bias=v, scale=-1.0)
-        t_acc = act([t_sg], T.sg[:, S + 128:S + 256], T.sg[:, S:S + 128], AF.Sign, bias=0.5, scale=-1.0, accum_out=acc)
-        for k in range(2):
-            t_c2 = ts([t_x, t_pb2] if k else [t_ro, t_vs], T.cm2[:, S + 128 * k:S + 128 * k + 128], T.ro[:, slot[k]], v,
-                      2.0, OP.is_ge, OP.mult)
-        for h, back in enumerate((T.bh, T.bl)):
-            t_p = scan([t_ne], T.pos[:, S + 128 * h:S + 128 * h + 128], T.ne[:, row], back[:], 0.0, OP.mult, OP.add)
-            t_lo = act([t_p], T.ab[:, 512 + 8 * h:518 + 8 * h:5], T.zero[:], AF.Identity,
-                       bias=T.pos[:, S + 128 * h + 127:S + 128 * h + 128])
-        if b:
-            store(b - 1, 1, "S")
-        else:
-            t_xp = reorder(2)
-        t_r2 = scan([t_c2], T.r2[:, row], T.cm2[:, S:S + 128], T.cm2[:, S + 128:S + 256], T.at2[:], OP.add, OP.add)
-        rk = T.r2[:, B + 127:B + 128]
-        if b:
-            t_st = tt([t_q], T.st[:, i:i + 4] if b < R - 1 else T.sf[:, 0:4], T.mq4[:, i:i + 4], T.st[:, i - 4:i], OP.add)
-        else:
-            fill(T.ab[:, 3:512:4], 0.0)
+            piece = ["turn%d " % c for c in range(4)]
+            for c in range(4):
+                D = C + 128 * c
+                sc = T.mx[:, D + 96:D + 97]
+                for name, j0, j1, op in (("lo", 0, c, OP.is_le), ("hi", c + 1, 4, OP.is_lt)):
+                    if (name, c) == ("lo", 1):
+                        act("sl", "mx1 turn0", T.sl[:, H:H + 32], T.srt[:, blk[0]], AF.Sign, bias=sc, scale=-1.0)
+                        act("lo1", "sl", T.sl[:, H + 32:H + 64], T.sl[:, H:H + 32], AF.Sign, bias=1.0,
+                            accum_out=T.cl[:, b:b + 1])
+                    elif j1 > j0:
+                        ts("%s%d" % (name, c), "mx%d " % c + "".join(piece[j0:j1]), T.cmp[:, D + 32 * j0:D + 32 * j1],
+                           T.srt[:, B + 32 * j0:B + 32 * j1], sc, None, op)
+                act("th%d" % c, "strict! dd%d" % c, T.th[:, blk[c]], T.strict[:], AF.Identity, bias=sc,
+                    scale=T.dd[:, i + c:i + c + 1])
+                tt("tt%d" % c, piece[c] + "th%d" % c, T.cmp[:, D + 32 * c:D + 32 * c + 32], T.srt[:, blk[c]],
+                   T.th[:, blk[c]], OP.is_le)
+                w = 16 if c == 1 else 0
+                scan("rs%d" % c, "tt%d" % c + " lo%d" % c * (c > 0) + " hi%d" % c * (c < 3),
+                     T.rs[:, S + 64 * c + w:S + 64 * c + 64], T.cmp[:, D + 2 * w:D + 64 + w], T.cmp[:, D + 64 + w:D + 128],
+                     T.cl[:, b:b + 1] if w else 0.0, OP.add, OP.add)
+                ts("ev%d" % c, "rs%d nz i32!" % c, T.ev[:, blk[c]], T.i32[:], T.rs[:, S + 64 * c + 63:S + 64 * c + 64],
+                   T.nz[:, i + c:i + c + 1], OP.is_equal, OP.mult)
+            for h in range(2):
+                turn("evt%d" % h, "ev%d ev%d" % (2 * h, 2 * h + 1), T.evt[:, B + 64 * h:B + 64 * h + 64],
+                     T.ev[:, B + 64 * h:B + 64 * h + 64])
+            scan("vs", "evt0 evt1", T.vs[:, H:H + 64], T.evt[:, B:B + 64], T.evt[:, B + 64:B + 128], 0.0, OP.add, OP.add)
+            ts("ne", "evt0 evt1", T.ne[:, row], T.evt[:, row], 0.0, None, OP.is_equal)
 
-        for h in range(2):
-            t_a = ts([t_i16, t_acc, t_r2], T.ab[:, h:512:4], T.i16[:, 128 * h:128 * h + 128], rk, acc, OP.subtract,
-                     OP.is_equal)
+            slot = [slice(G + 128 * k, G + 128 * k + 128) for k in range(3)]
+            rows = "".join(piece)
+            spread("pb0", rows, T.ro[:, slot[0]], T.srt[0:1, row], 128)
+            spread("pb1", rows, T.ro[0:96, slot[2]], T.srt[96:97, row], 96)
+            for n, (a, k, src) in enumerate(((2, 1, 1), (3, 1, 1), (3, 2, 2), (0, 1, 2), (1, 1, 2), (0, 0, 1))):
+                act("ro%d" % n, rows + ("" if k else "pb0"), T.ro[quad[a], slot[k]], T.srt[quad[src], row], AF.Identity,
+                    bias=TINY if k == 1 else 0.0)
+            v, acc = T.vs[:, H + 63:H + 64], T.acc[:, b:b + 1]
+            act("sg", "vs ro0 ro1 ro3 ro4", T.sg[:, S:S + 128], T.ro[:, slot[1]], AF.Sign, bias=v, scale=-1.0)
+            act("acc", "sg side!", T.sg[:, S + 128:S + 256], T.sg[:, S:S + 128], AF.Sign, bias=T.side[:], accum_out=acc)
+            for k in range(2):
+                ts("c2%d" % k, "vs epn! " + ("pb1 ro2" if k else "pb0 ro5"), T.cm2[:, S + 128 * k:S + 128 * k + 128],
+                   T.ro[:, slot[2 * k]], v, T.epn[:, 2 * k:2 * k + 1], OP.subtract, OP.is_le)
+            scan("r2", "c20 c21 at3!", T.r2[:, row], T.cm2[:, S:S + 128], T.cm2[:, S + 128:S + 256], T.at[:, 1:2],
+                 OP.add, OP.add)
+            rk = T.r2[:, B + 127:B + 128]
+
+            for h, back in enumerate((T.bh, T.bl)):
+                scan("pos%d" % h, "ne " + ("blz! bls!" if h else "bh0! bh1! bh2! bh3! bhs!"),
+                     T.pos[:, S + 128 * h:S + 128 * h + 128], T.ne[:, row], back[:], 0.0, OP.mult, OP.add)
+                act("b%d" % h, "pos%d zero! abz! l0-" % h, T.ab[:, 512 + 8 * h:518 + 8 * h:5], T.zero[:], AF.Identity,
+                    bias=T.pos[:, S + 128 * h + 127:S + 128 * h + 128])
+                ts("a%d" % h, "i16! acc r2", T.ab[:, h:512:4], T.i16[:, 128 * h:128 * h + 128], rk, acc, OP.subtract,
+                   OP.is_equal)
+            quant("abq", "a0 a1 b0 b1 ab2! ab3! l0-", T.abq, T.abs, 0, LW, T.ab, 0)
+            mm("l0", "abq off0- off1-", T.psr[:, 0:128], 0, T.abq, T.abs, 4, T.abq, T.abs)
+            for h in range(2):
+                ts("off%d" % h, "l0", T.off[:, 2 * b + h:2 * b + h + 1], T.psr[:, 124 + h:125 + h],
+                   T.psr[:, 126 + h:127 + h], 16.0, OP.add, OP.add)
+
+        off = T.off[:, 2 * b:2 * b + 2]
+        m0 = place(b, rank, rank)
+        cp("pick", "off0 off1", T.mq[:, m0:m0 + K].bitcast(dt.uint32), T.xq[:, 0:P].bitcast(dt.uint32).indirect(off))
+        act("psc", "off0 off1", T.ms[:, m0:m0 + K], T.xs[:, 0:P].indirect(off), AF.Copy)
+        send("sq", "pick", T.mq, b, True)
+        send("ss", "psc", T.ms, b, False)
+        act("ch", "off0 off1 num!", T.chs[:, K * b:K * b + K], T.num[:, 0:P].indirect(off), AF.Copy)
         if b < R - 1:
-            t_fl = ts([], T.fl[:, 32 * b:32 * b + 32], T.lim[:], rk, acc, OP.subtract, OP.is_gt)
+            if b:
+                f = slice(32 * b, 32 * b + 32)
+                ts("fl", "lim! acc r2", T.fl[:, f], T.lim[:], rk, acc, OP.subtract, OP.is_gt)
+                turn("flt", "fl", T.flt[:, f], T.fl[:, f])
+                red("cnt", "flt", T.cnt[:, b:b + 1], T.flt[:, f], OP.add)
+                ts("pen", "cnt rs0 rs1 rs2 rs3", T.pen[:, i:i + 4], T.rs[:, S + 63:S + 256:64], T.cnt[:, b:b + 1], GONE,
+                   OP.is_lt, OP.mult)
+                tt("srp", "pen st", T.old[:, 96:P:128], ranked, T.pen[:, i:i + 4], OP.add)
+            for c in range(4):
+                mm("own%d" % c, "pick psc pq%d!" % (c // 2), T.psc[:, 512 * c:512 * c + 128], 128 * c,
+                   T.pq, T.ps, m0 + K - 128, T.mq, T.ms)
+                red("mo%d" % c, "own%d" % c, T.mo[:, i + c:i + c + 1], T.psc[:, 512 * c + 128 - K:512 * c + 128], OP.max)
         else:
-            t_sft = turn([t_st], T.sft[:], T.sf[:])
+            ts("sq4", "st sf!", T.sf[:, 0:4], T.st[:, i:i + 4], -0.25, None, OP.mult)
+            turn("sft", "sq4", T.sft[:], T.sf[:])
             for a in range(4):
                 j = 128 * PIECE[a]
-                outs.append(dma("Y", T.se[0:1, j:j + 128], T.sft[32 * a:32 * a + 4, :], "dout", [t_sft]))
-        t_abq = quant([t_lo, t_a], T.abq, T.abs, 0, LW, T.ab, 0)
-        mm([t_abq], T.psr[:, 0:128], 0, T.abq, T.abs, 2, T.abq, T.abs, 128, True, False)
-        t_l = mm([], T.psr[:, 0:128], 0, T.abq, T.abs, 4, T.abq, T.abs, 128, False, True)
-        if b < R - 1:
-            t_flt = turn([t_fl], T.flt[:, 32 * b:32 * b + 32], T.fl[:, 32 * b:32 * b + 32])
-            if b == 0:
-                t_xv = reorder(3, True)
-            t_cnt = red([t_flt], T.cnt[:, b:b + 1], T.flt[:, 32 * b:32 * b + 32], OP.add)
-        off = T.off[:, 2 * b:2 * b + 2]
-        t_off = ts([t_l], off, T.psr[:, 126:128], 16.0, None, OP.add)
-        if b < R - 1:
-            t_pen = ts([t_cnt], T.pen[:, i:i + 4], T.rs[:, S + 63:S + 256:64], T.cnt[:, b:b + 1], GONE, OP.is_lt, OP.mult)
+                dma("se%d" % a, "Y", "sft", T.se[0:1, j:j + 128], T.sft[32 * a:32 * a + 4, :], "dout")
 
-        m0 = place(b, rank, rank)
-        t_pk = cp([t_off], T.mq[:, m0:m0 + K].bitcast(dt.uint32), T.xq[:, 0:P].bitcast(dt.uint32).indirect(off))
-        t_psc = act([t_off], T.ms[:, m0:m0 + K], T.xs[:, 0:P].indirect(off), AF.Copy)
-        need("G", [t_pk])
-        send(T.mq, b, True)
-        need("G", [t_psc])
-        send(T.ms, b, False)
+    lines = {e: [(w, b) for b in range(R + 1) for w in (FIRST if b == 0 else LATER if b < R else LAST)[e].split()
+                 if (w, b) in calls] for e in queue}
+    count, token, seen = {}, {}, {}
+    for key in [k for e in queue for k in lines[e]] + [("arr", b) for b in range(1, R + 1)]:
+        sem, n = calls[key][3:]
+        count[sem] = count.get(sem, 0) + n
+        token[key] = (sem, count[sem])
+    assert len(token) == len(calls)
 
-        t_ch = act([t_num], T.chs[:, K * b:K * b + K], T.num[:, 0:P].indirect(off), AF.Copy)
-        if b == 0:
-            t_pq = [quant([t_xp, t_xv], T.pq, T.ps, 256 * h, 256, T.xp, 1024 * h) for h in range(2)]
-        if b < R - 1:
-            t_own = [mm([t_pk, t_psc, t_pq[c // 2]], T.psc[:, 512 * c:512 * c + 128], 128 * c, T.pq, T.ps, m0 + K - 128,
-                        T.mq, T.ms, 128) for c in range(4)]
-            t_srp = tt([t_pen], T.srp[:, i:i + 4], T.bc[:, B:B + 128:32], T.pen[:, i:i + 4], OP.add)
-            if b == 0:
-                t_st = cp([], T.st[:, 0:4], T.bc[:, 0:128:32])
-                fill(T.quart[:], -0.25)
-                fill(T.low[:], LOW)
-            t_mo = [red([t_own[c]], T.mo[:, i + c:i + c + 1], T.psc[:, 512 * c + 128 - K:512 * c + 128], OP.max)
-                    for c in range(4)]
-            if b == 0:
-                t_wq = quant([dw], T.wq, T.ws, 0, 128 * O, T.wr, 0)
-                fill(T.sf[:], 0.0)
-        else:
-            outs.append(dma("Y", T.ch[:], T.chs[0:1, :], "dout", [t_ch]))
+    def need(e, sem, v):
+        if seen.get((e, sem), 0) < v:
+            queue[e].wait_ge(T.sem[sem], v)
+            seen[(e, sem)] = v
 
-        arrived = [t_pk, t_psc, ("arr%d" % b, (N - 1) * 2 * engs)]
-        M = UW + 128 * b
-        if b < R - 1:
-            t_mm = [mm([t_mo[3]] + arrived, T.psc[:, 512 * c:512 * c + 128], 128 * c, T.pq, T.ps, M, T.mq, T.ms, 128)
-                    for c in range(4)]
-            nb = B + 128
-            t_b4 = [None] * 4
-            for c in range(4):
-                X = 384 * b + 96 * c
-                t_m = scan([t_mo[3], t_mm[c]], T.mx[:, X:X + 96], T.psc[:, 512 * c + K:512 * c + 128], T.low[:],
-                           T.mo[:, i + c:i + c + 1], OP.max, OP.max)
-                t_b4[c] = act([t_m], T.bc[:, nb + 32 * c:nb + 32 * c + 32], T.quart[:], AF.Identity,
-                              bias=T.srp[:, i + c:i + c + 1], scale=T.mx[:, X + 95:X + 96])
-            t_srt = [turn([t_b4[c]], T.srt[:, nb + 32 * c:nb + 32 * c + 32], T.bc[:, nb + 32 * c:nb + 32 * c + 32])
-                     for c in range(4)]
-        for o in (1, 0):
-            t_y[o] = mm([t_wq] + [t for t in free_y if t] + arrived, psy[o], 128 * o, T.wq, T.ws, M, T.mq, T.ms, 128)
-        if b == R - 1:
-            store(b, 1, "S")
-            store(b, 0, "V")
-
-    need("Y", [outs[-1]])
-    need("G", [("loc", 2 * R * engs)])
-    for s in ("sv", "ss", "sp", "sg"):
-        need("Y", [(s, count[s])])
+    for e in queue:
+        for key in lines[e]:
+            _, keys, issue, sem, n = calls[key]
+            if sem == "sg":
+                need(e, sem, token[key][1] - 1)
+            for s in sorted(set(token[k][0] for k in keys)):
+                need(e, s, max(token[k][1] for k in keys if token[k][0] == s))
+            ins = issue()
+            if sem != "loc":
+                ins.then_inc(T.sem[sem], n)
+    need("G", "loc", count["loc"])
+    for s in ("dout", "sv", "ss", "sp", "sg"):
+        need("Y", s, count[s])

from concourse.bass import DstId, RemoteDMATransfer
from concourse.mybir import dt, AluOpType, AxisListType, ActivationFunctionType

OP = AluOpType
P, K, R, O, N = 512, 32, 4, 2, 4
PIECE = (3, 2, 1, 0)
UW = 128
LW = 132
FW = 262
SCALAR = {0: 3, 1: 3, 2: 3, 3: 2}
KAPPA = 2.0 ** -24 * (1.0 + 2.0 ** -10)
TINY = 2.0 ** -124
FLOOR = -2.0 ** 90
GONE = 1e29


def _sbuf(dtype, **widths):
    return {name: ("sbuf", [128, w], dtype) for name, w in widths.items()}


SCRATCH = {
    **_sbuf("bfloat16", uc=4, ones=128, ut=4 * UW, xr=4 * P, xp=4 * P, wr=512 * O, i32=32, i16=256, lim=32, cmp=P * R,
            jp=128, tri=128, dg=P, sl=64 * R, ne=128 * R, cm2=256 * R, sg=256 * R, bh=128, bl=128, pos=256 * R,
            ab=4 * LW, fl=32 * R, flt=32 * R, f0=4 * P, s0=256 * 4, r0=256 * 4, a0=4 * (FW + 32)),
    **_sbuf("float8_e4m3fn_x4", xq=P, pq=P, wq=128 * O, mq=UW + 128 * R, abq=LW, q0=FW, fq=160),
    **_sbuf("uint8", xs=P, ps=P, ws=128 * O, ms=UW + 128 * R, abs=LW, p0=FW, fs=160),
    **_sbuf("float32", old=2 * P, strict=32, num=P, at=2, ei=4, epn=3, side=1, a32=1, zero=2,
            sc=4, pr=8, srt=128 * R, th=128 * R, dd=4 * R, nz=4 * R, rs=256 * R, ev=128 * R, evt=128 * R,
            vs=64 * R, r2=128 * R, ro=384 * R, acc=R, cl=R, c0=4, chs=K * R, cnt=R, pen=4 * R, mo=4 * R, mx=P * R,
            st=4 * R, sf=32, sft=32, ysb=O * P),
    **_sbuf("uint16", off=2 * R),
    "psc": ("psum", [128, 2048], "float32"),
    "psr": ("psum", [128, 2048], "float32"),
}
SEMAPHORES = ["sv", "ss", "sp", "sg", "du", "dx0", "dx1", "dx2", "dx3", "dp0", "dp1", "dw", "dout",
              "arr0", "arr1", "arr2", "arr3", "loc"]

FIRST = {
    "V": "ones old bh0 bh1 bh2 bh3 blz sf tri xq0 ut0 ut1 ut2 uq xq1 xq2 xq3 a32 u10 strict tt0 u01 tt1 u20 u02 u12 "
         "u21 u30 u31 tt2 rs0 tt3 rs1 a00 rs2 a01 rs3 a10 a11 a20 a21 a30 a31 "
         "pen t0 abq abf t1 bhs bls off0 off1 ab2 pick pq0 pq1 wq mo0 mo1 mo2 mo3 ab3",
    "S": "dx0 dx2 zero abz lim bh bl side epn ut3 az hold sc0 sc1 dg0 dg1 sc2 sc3 dg2 sg0 sg1 sg2 dg3 acc0 sg3 "
         "acc1 acc2 acc3 lo hi tr00 tr10 tr20 tr30 tr01 tr11 tr21 tr31 psc ch tr02 tr12 tr22 tr32 tr03 tr13 tr23 tr33",
    "P": "col0 col1 dup0 dup1 row0 row1 col2 col3 dup2 dup3 row2 l0 l1 fm0 fm1 fm2 fm3 own0 own1 own2 own3",
    "G": "jp ei at0 at1 at2 at3 i32 i16 num sq ss",
    "Y": "du dx1 dx3 re00 re10 re20 re30 re01 re11 re21 re31 re02 re12 re22 re32 re03 re13 re23 re33 dw",
}
LATER = {
    "V": "mx0 mx1 mx2 mx3 turn0 turn1 turn2 turn3 lo2 lo3 tt0 hi0 tt1 hi1 hi2 tt2 tt3 rs0 rs1 rs2 rs3 "
         "ev0 ev1 ev2 ev3 evt0 st evt1 yc1 vs ne sq4 c20 c21 pos0 pos1 sft r2 a0 a1 fl abq flt off0 off1 cnt pick "
         "pen srp mo0 mo1 mo2 mo3",
    "S": "dd0 dd1 dd2 th0 dd3 th1 sl th2 th3 lo1 nz ro0 ro1 ro2 ro3 ro4 ro5 yc0 sg acc b0 b1 psc ch",
    "P": "mm0 mm1 mm2 mm3 ym1 ym0 l0 own0 own1 own2 own3",
    "G": "pb0 pb1 sq ss",
    "Y": "yd0 ye0 yd1 ye1 se0 se1 se2 se3",
}
LAST = {"V": "yc0", "S": "yc1 yd1", "P": "ym1 ym0", "G": "", "Y": "dch yd0"}


def rank_program(g, core, T, topo):
    rank = T.rank_of(core)
    if rank is None:
        return
    AF = ActivationFunctionType
    queue = {"V": g.vector, "S": g.scalar, "P": g.tensor, "G": g, "Y": g.sync}
    own = {"V": "sv", "S": "ss", "P": "sp", "G": "sg"}
    V, calls, now = g.vector, {}, [0]

    def call(name, e, needs, issue, sem=None, n=1):
        keys = []
        for w in needs.split():
            keys.append((w[:-1], now[0] - 1) if w[-1] == "-" else (w[:-1], 0) if w[-1] == "!" else (w, now[0]))
        calls[(name, now[0])] = (e, keys, issue, sem or own[e], n)

    def dma(name, e, needs, out, in_, sem):
        call(name, e, needs, lambda: queue[e].dma_start(out, in_), sem, 16)

    def ts(name, needs, out, in0, s1, s2, *ops):
        call(name, "V", needs, lambda: V.tensor_scalar(out, in0, s1, s2, *ops))

    def tt(name, needs, out, in0, in1, op):
        call(name, "V", needs, lambda: V.tensor_tensor(out, in0, in1, op))

    def cp(name, needs, out, in_):
        call(name, "V", needs, lambda: V.tensor_copy(out, in_))

    def turn(name, needs, out, in_):
        call(name, "V", needs, lambda: V.transpose(out, in_))

    def scan(name, needs, out, d0, d1, init, op0, op1):
        call(name, "V", needs, lambda: V.tensor_tensor_scan(out, d0, d1, init, op0, op1))

    def red(name, needs, out, in_, op):
        call(name, "V", needs, lambda: V.tensor_reduce(out, in_, AxisListType.X, op))

    def act(name, needs, out, in_, func, **kw):
        call(name, "S", needs, lambda: g.scalar.activation(out, in_, func, **kw))

    def fill(name, ap, v, needs=""):
        call(name, "V", needs, lambda: V.memset(ap, v))

    def whole(name, out, pattern, step, start=0):
        call(name, "G", "", lambda: g.iota(out, pattern, start, step, allow_small_or_imprecise_dtypes=True))

    def spread(name, needs, out, in_, channels):
        call(name, "G", needs, lambda: g.partition_broadcast(out, in_, channels))

    def quant(name, needs, q, s, a, n, src, sa):
        call(name, "V", needs, lambda: V.quantize_mx(q[:, a:a + n], s[:, a:a + n], src[:, sa:sa + 4 * n]))

    def mm(name, needs, out, l, lq, ls, r, rq, rs, start=True, stop=True):
        n = out.shape[1]
        call(name, "P", needs, lambda: g.tensor.matmul_mx(out, lq[:, l:l + 128], ls[:, l:l + 128],
                                                          rq[:, r:r + n], rs[:, r:r + n], start, stop))

    quad = [slice(32 * a, 32 * a + 32) for a in range(4)]

    dma("du", "Y", "", T.uc[:], T.u[:, 0:4], "du")
    for j in range(4):
        dma("dx%d" % j, "SYSY"[j], "", T.xr[:, 512 * j:512 * j + 512], T.x[:, 512 * j:512 * j + 512], "dx%d" % j)
    for a in range(4):
        for c in range(4):
            j = 512 * PIECE[a] + 128 * c
            dma("re%d%d" % (a, c), "Y", "dx0 dx1 dx2 dx3", T.xp[:, 512 * c + 128 * a:512 * c + 128 * a + 128],
                T.x[:, j:j + 128], "dp%d" % (c // 2))
    dma("dw", "Y", "", T.wr[:], T.w[:], "dw")
    for h in range(2):
        quant("pq%d" % h, " ".join("re%d%d" % (a, c) for a in range(4) for c in (2 * h, 2 * h + 1)),
              T.pq, T.ps, 256 * h, 256, T.xp, 1024 * h)
    quant("wq", "dw", T.wq, T.ws, 0, 128 * O, T.wr, 0)

    fill("ones", T.ones[:], 1.0)
    for t in range(3):
        ts("ut%d" % t, "du ones", T.ut[:, t:512:4], T.ones[:], T.uc[:, t:t + 1], None, OP.mult)
    act("ut3", "du ones", T.ut[:, 3:512:4], T.ones[:], AF.Identity, bias=T.uc[:, 3:4], scale=0.0)
    quant("uq", "ut0 ut1 ut2 ut3", T.mq, T.ms, 0, 128, T.ut, 0)

    for name, out, v in (("zero", T.zero[:], 0.0), ("abz", T.ab[:, 512:4 * LW], 0.0),
                         ("az", T.a0[:, 1024:4 * FW], 0.0), ("hold", T.a0[:, 4 * FW:4 * FW + 128], FLOOR),
                         ("lim", T.lim[:], float(K)), ("bh", T.bh[:, 0:127], 0.0), ("bl", T.bl[:, 0:127], -1.0)):
        act(name, "ones", out, T.ones[:, 0:out.shape[1]], AF.Identity, scale=v)
    for a in range(4):
        whole("at%d" % a, T.at[quad[a], :], [[128 * (a // 2), 2]], 1)
        fill("bh%d" % a, T.bh[quad[a], 127:128], 128.0 * PIECE[a] + 96)
    whole("i32", T.i32[:], [[1, 32]], 0)
    whole("i16", T.i16[:], [[16, 2], [0, 8], [1, 16]], 0)
    whole("ei", T.ei[:], [[-32, 4]], 1)
    whole("num", T.num[:], [[1, P]], 0)
    fill("blz", T.bl[:, 127:128], 15.0)
    fill("bhs", T.bh[:, 31:96:32], -32.0, "bh")
    fill("bls", T.bl[:, 31:96:32], 31.0, "bl")
    for t in (2, 3):
        fill("ab%d" % t, T.ab[:, t:512:4], 0.0)
    fill("old", T.old[:, 0:P], 0.0)
    fill("sf", T.sf[:], 0.0)
    whole("jp", T.jp[:], [[1, 128]], -1)
    ts("tri", "jp", T.tri[:], T.jp[:], 0.0, TINY, OP.is_lt, OP.mult)
    ts("strict", "i32 at3", T.strict[:], T.i32[:], T.at[:, 0:1], -1.0, OP.is_ge, OP.mult)
    act("side", "ei", T.side[:], T.ei[:, 2:3], AF.Sign, bias=-0.5, scale=-1.0)
    act("epn", "ei", T.epn[:], T.ei[:, 1:4], AF.Identity, bias=-2 * TINY, scale=-4 * TINY)
    ts("a32", "ei at3", T.a32[:], T.ei[:, 0:1], T.at[:, 0:1], None, OP.subtract)
    act("hi", "az i32 a32", T.a0[:, 1032:1036], T.i32[:, 0:4], AF.Identity, bias=T.a32[:], scale=128.0)
    act("lo", "az at3", T.a0[:, 1036:1040], T.ones[:, 0:4], AF.Identity, bias=T.at[:, 0:1], scale=-16.0)

    rows0 = [T.psc[:, 512 * j:512 * j + 128] for j in range(4)]
    for c in range(4):
        E, z = 512 * c, 512 * (c % 2)
        twin = T.psr[:, 1024 + z:1152 + z]
        quant("xq%d" % c, "dx%d" % c, T.xq, T.xs, 128 * c, 128, T.xr, 512 * c)
        mm("col%d" % c, "uq xq%d" % c + " sc%d" % (c - 2) * (c > 1), T.psr[:, z:z + 128], 128 * c, T.xq, T.xs,
           0, T.mq, T.ms)
        if c < 3:
            mm("row%d" % c, "uq xq%d" % c, rows0[c], 0, T.mq, T.ms, 128 * c, T.xq, T.xs)
        mm("dup%d" % c, "uq xq%d" % c + " dg%d" % (c - 2) * (c > 1), twin, 0, T.mq, T.ms, 128 * c, T.xq, T.xs)
        sc = T.sc[:, c:c + 1]
        act("sc%d" % c, "col%d" % c, sc, T.psr[:, z:z + 1], AF.Copy)
        act("dg%d" % c, "sc%d dup%d" % (c, c), T.dg[:, 128 * c:128 * c + 128], twin, AF.Identity, bias=sc, scale=-1.0)
        tt("tt%d" % c, "tri dg%d" % c, T.f0[:, E:E + 128], T.dg[:, 128 * c:128 * c + 128], T.tri[:], OP.is_lt)
        n, needs = 128, "tt%d" % c
        for j in range(4):
            if j == SCALAR.get(c):
                sign, count = T.s0[:, 256 * c:256 * c + 128], T.s0[:, 256 * c + 128:256 * c + 256]
                act("sg%d" % c, "sc%d dup%d" % (c, j), sign, T.psr[:, 512 * j:512 * j + 128], AF.Sign, bias=sc, scale=-1.0)
                act("acc%d" % c, "sg%d" % c, count, sign, AF.Sign if j < c else AF.Relu, bias=float(j < c), scale=-1.0,
                    accum_out=T.c0[:, c:c + 1])
                needs += " acc%d" % c
            elif j != c:
                ts("u%d%d" % (c, j), "sc%d row%d" % (c, j), T.f0[:, E + n:E + n + 128], rows0[j], sc, None,
                   OP.is_ge if j < c else OP.is_gt)
                n, needs = n + 128, needs + " u%d%d" % (c, j)
        end = 256 * c + 256
        scan("rs%d" % c, needs, T.r0[:, end - n // 2:end], T.f0[:, E:E + n // 2], T.f0[:, E + n // 2:E + n],
             T.c0[:, c:c + 1] if c in SCALAR else 0.0, OP.add, OP.add)
        for h in range(2):
            ts("a%d%d" % (c, h), "i16 rs%d" % c, T.a0[:, 512 * h + c:512 * h + 512:4], T.i16[:, 128 * h:128 * h + 128],
               T.r0[:, end - 1:end], None, OP.is_equal)
        mm("fm%d" % c, "abf abq", T.psc[:, 512 * c:512 * c + 160], 0, T.q0, T.p0, 0, T.fq, T.fs)
    every = " ".join("a%d%d" % (c, h) for c in range(4) for h in range(2))
    quant("abq", every + " hi lo", T.q0, T.p0, 0, FW, T.a0, 0)
    quant("abf", every + " hi lo hold", T.fq, T.fs, 0, 160, T.a0, 4 * (FW - 128))
    for h in range(2):
        mm("l%d" % h, "abq", T.psr[:, 0:128], 128 * h, T.q0, T.p0, FW - 128 - 2 * h, T.q0, T.p0, h == 0, h == 1)
        ts("off%d" % h, "l1", T.off[:, h:h + 1], T.psr[:, 124 + 2 * h:125 + 2 * h], T.psr[:, 125 + 2 * h:126 + 2 * h], 16.0,
           OP.add, OP.add)
    ts("pen", "rs0 rs1 rs2 rs3", T.pen[:, 0:4], T.r0[:, 255:1024:256], float(K), GONE, OP.is_lt, OP.mult)
    ts("t0", "sc0 sc1 sc2 sc3", T.pr[:, 1:8:2], T.sc[:], -4.0, None, OP.mult)
    tt("t1", "pen t0", T.pr[:, 0:8:2], T.pr[:, 1:8:2], T.pen[:, 0:4], OP.add)
    for a in range(4):
        for c in range(4):
            act("tr%d%d" % (a, c), "t1 old", T.old[quad[a], 128 * c + 96:128 * c + 96 + P + 1:P],
                T.pr[quad[c], 2 * PIECE[a]:2 * PIECE[a] + 2], AF.Copy)

    dests = [T.cores[(rank + k) % N] for k in range(1, N)]
    mask = topo.mask(core, dests[0])
    ids = []
    for c in dests:
        mask &= topo.mask(core, c)
        rid, pid, _ = topo.addr(c)
        ids.append(DstId(rid=rid, pnc=pid))
    engs = bin(mask).count("1")
    usable = [e for e in topo.engines(core, dests[0]) if mask >> e & 1]
    halves = [sum(1 << e for e in usable[k::2]) for k in range(2)]

    def place(b, sender, holder):
        return UW + 128 * b + K * ((sender - holder) % N if b < R - 1 else sender)

    def send(name, needs, buf, b, codes):
        views = [buf[:, place(b, rank, T.rank_of(c)):place(b, rank, T.rank_of(c)) + K] for c in [core] + dests]
        if codes:
            views = [v.bitcast(dt.uint8) for v in views]
        m = halves[0 if codes else 1] if b == 0 else mask
        call(name, "G", needs, lambda: g.remote_dma_fused(
            [RemoteDMATransfer(dst_ids=ids, dma_engine_mask=m, remote_sem=T.sem["arr%d" % b], srcs=views[:1],
                               dsts=views[1:])], local_sem=T.sem.loc), "loc", bin(m).count("1"))

    psy = [T.psr[:, 512 + 512 * o:512 + 512 * o + 128] for o in range(O)]

    for b in range(R + 1):
        now[0] = b
        B, C, i, G, S, H = 128 * b, P * b, 4 * b, 384 * b, 256 * b, 64 * b
        row = slice(B, B + 128)
        blk = [slice(B + 32 * c, B + 32 * c + 32) for c in range(4)]
        if b:
            calls[("arr", b)] = (None, [], None, "arr%d" % (b - 1), (N - 1) * (2 if b > 1 else 1) * engs)
            M = UW + B - 128
            for o in range(O):
                mm("ym%d" % o, "arr pick- psc- wq!" + (" yc%d-" % o if b > 1 else ""), psy[o], 128 * o, T.wq, T.ws,
                   M, T.mq, T.ms)
                c0 = P * o + B - 128
                out = T.ysb[:, c0:c0 + 128]
                if "yc%d" % o in (LATER if b < R else LAST)["V"]:
                    cp("yc%d" % o, "ym%d" % o, out, psy[o])
                else:
                    act("yc%d" % o, "ym%d" % o, out, psy[o], AF.Copy)
                cut = K * rank if b < R else 0
                e = "Y" if b < R or o == 0 else "S"
                dma("yd%d" % o, e, "yc%d" % o, T.y[:, c0 + cut:c0 + 128], T.ysb[:, c0:c0 + 128 - cut], "dout")
                if cut:
                    dma("ye%d" % o, e, "yc%d" % o, T.y[:, c0:c0 + cut], T.ysb[:, c0 + 128 - cut:c0 + 128], "dout")
            if b == R:
                dma("dch", "Y", "arr ch-", T.ch[:], T.chs[0:1, :], "dout")
                break
            for c in range(4):
                X = C + 128 * c
                placed = "srp-" if b > 1 else " ".join("tr%d%d-" % (a, c) for a in range(4))
                mm("mm%d" % c, "arr mo%d-" % c, T.psc[:, 512 * c:512 * c + 128], 128 * c, T.pq, T.ps, M, T.mq, T.ms)
                scan("mx%d" % c, "mm%d " % c + placed, T.mx[:, X:X + 128], T.psc[:, 512 * c + K:512 * c + 160],
                     T.old[:, 128 * c:128 * c + 128], T.mo[:, i - 4 + c:i - 3 + c], OP.max, OP.add)
                act("dd%d" % c, "mx%d" % c, T.dd[:, i + c:i + c + 1], T.mx[:, X + 96:X + 97], AF.Abs, bias=TINY,
                    scale=KAPPA)
                turn("turn%d" % c, "mx%d" % c, T.srt[:, blk[c]], T.mx[:, X + 96:X + 128])
            ranked = T.mx[:, C + 96:C + P:128]
            act("nz", "mx0 mx1 mx2 mx3", T.nz[:, i:i + 4], ranked, AF.Identity, bias=TINY)
            tt("st", "mx0 mx1 mx2 mx3" + " st-" * (b > 1), T.st[:, i:i + 4], T.mx[:, C + 95:C + P:128],
               T.st[:, i - 4:i] if b > 1 else T.old[:, P + 96:2 * P:128], OP.add)

            piece = ["turn%d " % c for c in range(4)]
            for c in range(4):
                D = C + 128 * c
                sc = T.mx[:, D + 96:D + 97]
                for name, j0, j1, op in (("lo", 0, c, OP.is_le), ("hi", c + 1, 4, OP.is_lt)):
                    if (name, c) == ("lo", 1):
                        act("sl", "mx1 turn0", T.sl[:, H:H + 32], T.srt[:, blk[0]], AF.Sign, bias=sc, scale=-1.0)
                        act("lo1", "sl", T.sl[:, H + 32:H + 64], T.sl[:, H:H + 32], AF.Sign, bias=1.0,
                            accum_out=T.cl[:, b:b + 1])
                    elif j1 > j0:
                        ts("%s%d" % (name, c), "mx%d " % c + "".join(piece[j0:j1]), T.cmp[:, D + 32 * j0:D + 32 * j1],
                           T.srt[:, B + 32 * j0:B + 32 * j1], sc, None, op)
                act("th%d" % c, "strict! dd%d" % c, T.th[:, blk[c]], T.strict[:], AF.Identity, bias=sc,
                    scale=T.dd[:, i + c:i + c + 1])
                tt("tt%d" % c, piece[c] + "th%d" % c, T.cmp[:, D + 32 * c:D + 32 * c + 32], T.srt[:, blk[c]],
                   T.th[:, blk[c]], OP.is_le)
                w = 16 if c == 1 else 0
                scan("rs%d" % c, "tt%d" % c + " lo%d" % c * (c > 0) + " hi%d" % c * (c < 3),
                     T.rs[:, S + 64 * c + w:S + 64 * c + 64], T.cmp[:, D + 2 * w:D + 64 + w], T.cmp[:, D + 64 + w:D + 128],
                     T.cl[:, b:b + 1] if w else 0.0, OP.add, OP.add)
                ts("ev%d" % c, "rs%d nz i32!" % c, T.ev[:, blk[c]], T.i32[:], T.rs[:, S + 64 * c + 63:S + 64 * c + 64],
                   T.nz[:, i + c:i + c + 1], OP.is_equal, OP.mult)
            for h in range(2):
                turn("evt%d" % h, "ev%d ev%d" % (2 * h, 2 * h + 1), T.evt[:, B + 64 * h:B + 64 * h + 64],
                     T.ev[:, B + 64 * h:B + 64 * h + 64])
            scan("vs", "evt0 evt1", T.vs[:, H:H + 64], T.evt[:, B:B + 64], T.evt[:, B + 64:B + 128], 0.0, OP.add, OP.add)
            ts("ne", "evt0 evt1", T.ne[:, row], T.evt[:, row], 0.0, None, OP.is_equal)

            slot = [slice(G + 128 * k, G + 128 * k + 128) for k in range(3)]
            rows = "".join(piece)
            spread("pb0", rows, T.ro[:, slot[0]], T.srt[0:1, row], 128)
            spread("pb1", rows, T.ro[0:96, slot[2]], T.srt[96:97, row], 96)
            for n, (a, k, src) in enumerate(((2, 1, 1), (3, 1, 1), (3, 2, 2), (0, 1, 2), (1, 1, 2), (0, 0, 1))):
                act("ro%d" % n, rows + ("" if k else "pb0"), T.ro[quad[a], slot[k]], T.srt[quad[src], row], AF.Identity,
                    bias=TINY if k == 1 else 0.0)
            v, acc = T.vs[:, H + 63:H + 64], T.acc[:, b:b + 1]
            act("sg", "vs ro0 ro1 ro3 ro4", T.sg[:, S:S + 128], T.ro[:, slot[1]], AF.Sign, bias=v, scale=-1.0)
            act("acc", "sg side!", T.sg[:, S + 128:S + 256], T.sg[:, S:S + 128], AF.Sign, bias=T.side[:], accum_out=acc)
            for k in range(2):
                ts("c2%d" % k, "vs epn! " + ("pb1 ro2" if k else "pb0 ro5"), T.cm2[:, S + 128 * k:S + 128 * k + 128],
                   T.ro[:, slot[2 * k]], v, T.epn[:, 2 * k:2 * k + 1], OP.subtract, OP.is_le)
            scan("r2", "c20 c21 at3!", T.r2[:, row], T.cm2[:, S:S + 128], T.cm2[:, S + 128:S + 256], T.at[:, 1:2],
                 OP.add, OP.add)
            rk = T.r2[:, B + 127:B + 128]

            for h, back in enumerate((T.bh, T.bl)):
                scan("pos%d" % h, "ne " + ("blz! bls!" if h else "bh0! bh1! bh2! bh3! bhs!"),
                     T.pos[:, S + 128 * h:S + 128 * h + 128], T.ne[:, row], back[:], 0.0, OP.mult, OP.add)
                act("b%d" % h, "pos%d zero! abz! l0-" % h, T.ab[:, 512 + 8 * h:518 + 8 * h:5], T.zero[:], AF.Identity,
                    bias=T.pos[:, S + 128 * h + 127:S + 128 * h + 128])
                ts("a%d" % h, "i16! acc r2", T.ab[:, h:512:4], T.i16[:, 128 * h:128 * h + 128], rk, acc, OP.subtract,
                   OP.is_equal)
            quant("abq", "a0 a1 b0 b1 ab2! ab3! l0-", T.abq, T.abs, 0, LW, T.ab, 0)
            mm("l0", "abq off0- off1-", T.psr[:, 0:128], 0, T.abq, T.abs, 4, T.abq, T.abs)
            for h in range(2):
                ts("off%d" % h, "l0", T.off[:, 2 * b + h:2 * b + h + 1], T.psr[:, 124 + h:125 + h],
                   T.psr[:, 126 + h:127 + h], 16.0, OP.add, OP.add)

        off = T.off[:, 2 * b:2 * b + 2]
        m0 = place(b, rank, rank)
        cp("pick", "off0 off1", T.mq[:, m0:m0 + K].bitcast(dt.uint32), T.xq[:, 0:P].bitcast(dt.uint32).indirect(off))
        act("psc", "off0 off1", T.ms[:, m0:m0 + K], T.xs[:, 0:P].indirect(off), AF.Copy)
        send("sq", "pick", T.mq, b, True)
        send("ss", "psc", T.ms, b, False)
        act("ch", "off0 off1 num!", T.chs[:, K * b:K * b + K], T.num[:, 0:P].indirect(off), AF.Copy)
        if b < R - 1:
            if b:
                f = slice(32 * b, 32 * b + 32)
                ts("fl", "lim! acc r2", T.fl[:, f], T.lim[:], rk, acc, OP.subtract, OP.is_gt)
                turn("flt", "fl", T.flt[:, f], T.fl[:, f])
                red("cnt", "flt", T.cnt[:, b:b + 1], T.flt[:, f], OP.add)
                ts("pen", "cnt rs0 rs1 rs2 rs3", T.pen[:, i:i + 4], T.rs[:, S + 63:S + 256:64], T.cnt[:, b:b + 1], GONE,
                   OP.is_lt, OP.mult)
                tt("srp", "pen st", T.old[:, 96:P:128], ranked, T.pen[:, i:i + 4], OP.add)
            for c in range(4):
                mm("own%d" % c, "pick psc pq%d!" % (c // 2), T.psc[:, 512 * c:512 * c + 128], 128 * c,
                   T.pq, T.ps, m0 + K - 128, T.mq, T.ms)
                red("mo%d" % c, "own%d" % c, T.mo[:, i + c:i + c + 1], T.psc[:, 512 * c + 128 - K:512 * c + 128], OP.max)
        else:
            ts("sq4", "st sf!", T.sf[:, 0:4], T.st[:, i:i + 4], -0.25, None, OP.mult)
            turn("sft", "sq4", T.sft[:], T.sf[:])
            for a in range(4):
                j = 128 * PIECE[a]
                dma("se%d" % a, "Y", "sft", T.se[0:1, j:j + 128], T.sft[32 * a:32 * a + 4, :], "dout")

    lines = {e: [(w, b) for b in range(R + 1) for w in (FIRST if b == 0 else LATER if b < R else LAST)[e].split()
                 if (w, b) in calls] for e in queue}
    count, token, seen = {}, {}, {}
    for key in [k for e in queue for k in lines[e]] + [("arr", b) for b in range(1, R + 1)]:
        sem, n = calls[key][3:]
        count[sem] = count.get(sem, 0) + n
        token[key] = (sem, count[sem])
    assert len(token) == len(calls)

    def need(e, sem, v):
        if seen.get((e, sem), 0) < v:
            queue[e].wait_ge(T.sem[sem], v)
            seen[(e, sem)] = v

    for e in queue:
        for key in lines[e]:
            _, keys, issue, sem, n = calls[key]
            if sem == "sg":
                need(e, sem, token[key][1] - 1)
            for s in sorted(set(token[k][0] for k in keys)):
                need(e, s, max(token[k][1] for k in keys if token[k][0] == s))
            ins = issue()
            if sem != "loc":
                ins.then_inc(T.sem[sem], n)
    need("G", "loc", count["loc"])
    for s in ("dout", "sv", "ss", "sp", "sg"):
        need("Y", s, count[s])
